import numpy as np
import ml_dtypes


def mxq(x, axis, fmt="e4m3"):
    dtype, down = {"e4m3": (ml_dtypes.float8_e4m3fn, 7), "e5m2": (ml_dtypes.float8_e5m2, 14)}[fmt]
    v = np.moveaxis(np.asarray(x, np.float32).astype(ml_dtypes.bfloat16).astype(np.float64), axis, -1)
    blocks = v.reshape(v.shape[:-1] + (-1, 32))
    amax = np.abs(blocks).max(-1, keepdims=True)
    byte = np.maximum(np.where(amax > 0, np.frexp(amax)[1] - 1 + 127, 0) - down, 1)
    scale = np.exp2(byte - 127.0)
    codes = (blocks / scale).astype(np.float32).astype(dtype).astype(np.float64)
    return np.moveaxis((codes * scale).reshape(v.shape), -1, axis)


WIDE = False


def mx_kscale(k):
    if not WIDE:
        return np.ones(k)
    levels = np.array([10, -10, 5, -5, 0])
    if k % 512:
        return np.exp2(np.random.permutation(np.resize(levels, k // 32))).repeat(32)
    a = np.empty((k // 512, 16))
    for p in range(k // 512):
        a[p, :8] = np.random.permutation(np.resize(levels, 8))
        for g in range(8):
            far = levels[np.abs(levels - a[p, g]) >= 10]
            a[p, g + 8] = far[np.random.randint(len(far))]
    return np.exp2(a.ravel()).repeat(32)


def f64(x):
    return np.asarray(x).astype(np.float64)


def striped(idx):
    return np.tile(idx.reshape(-1, 16).T, (8, 1)).astype(np.uint16)


def unstriped(offs):
    return offs[:16].T.reshape(-1).astype(np.int64)


def pack_weight(w):
    k, n = w.shape
    w = f64(np.asarray(w, np.float32).astype(ml_dtypes.bfloat16)).reshape(k // 32, 32, n)
    amax = np.abs(w).max(1)
    byte = np.clip(np.where(amax > 0, np.frexp(amax)[1] - 1 + 127 - 7, 1), 1, 254)
    scaled = (w * np.exp2(127.0 - byte)[:, None, :]).reshape(k, n).astype(np.float32)
    words = np.ascontiguousarray(scaled.reshape(k // 512, 128, 4, n).transpose(0, 1, 3, 2)).astype(ml_dtypes.float8_e4m3fn).view(np.uint8)
    return words, np.ascontiguousarray(byte.astype(np.uint8).reshape(k // 512, 16, n))


def unpack_weight(words, scales):
    g, p, n, _ = words.shape
    vals = np.ascontiguousarray(words).view(ml_dtypes.float8_e4m3fn).astype(np.float64) * np.repeat(np.exp2(scales.astype(np.float64) - 127.0), 8, axis=1)[..., None]
    return vals.transpose(0, 1, 3, 2).reshape(g * 512, n)


def gelu(v):
    return 0.5 * v * (1.0 + np.tanh(np.sqrt(2.0 / np.pi) * (v + 0.044715 * v**3)))


K, T, S, H, N = 512, 2048, 1024, 512, 128
P = 2 ** 7


def setup_inputs():
    n = np.random.standard_normal
    s = mx_kscale(K)[:, None]
    u = mx_kscale(H)
    packed_xT = pack_weight(n((K, T)) * s)
    return {
        "x_words": packed_xT[0],
        "x_scales": packed_xT[1],
        "w1": (n((K, H)) / np.sqrt(K) / s * u).astype(np.float32),
        "w2": (n((H, N)) / np.sqrt(H) / u[:, None]).astype(np.float32),
        "lam": np.tile(np.random.uniform(0.1, 0.9, S), (P, 1)).astype(np.float32),
        "mu": np.tile(np.random.uniform(0.1, 0.9, S), (P, 1)).astype(np.float32),
        "offs": striped(np.random.permutation(T)[:S]),
        "pos1": striped(np.random.permutation(S)),
    }


def reference(x_words, x_scales, w1, w2, lam, mu, offs, pos1):
    xq = unpack_weight(x_words, x_scales)[:, unstriped(offs)]
    h = gelu(mxq(f64(w1), 0, "e4m3").T @ xq)
    z = h * f64(lam)[:1] + h[:, unstriped(pos1)] * f64(mu)[:1]
    return mxq(f64(w2), 0, "e4m3").T @ mxq(z, 0, "e4m3")

@@ -1,0 +1,198 @@
+from contextlib import ExitStack
+
+import concourse.mybir as mybir
+from concourse.masks import make_identity
+
+K, T, S, H, N = 512, 2048, 1024, 512, 128
+FLOPS = 2 * K * H * S + 2 * H * N * S
+BYTES = K * T + 16 * T + 4 * K * H + 4 * H * N + 2 * 4 * S + 2 * 2 * 128 * (S // 16) + 4 * N * S
+
+F32 = mybir.dt.float32
+BF16 = mybir.dt.bfloat16
+I32 = mybir.dt.int32
+U32 = mybir.dt.uint32
+U16 = mybir.dt.uint16
+U8 = mybir.dt.uint8
+FP8X4 = mybir.dt.float8_e4m3fn_x4
+ACT = mybir.ActivationFunctionType
+ALU = mybir.AluOpType
+
+P = 128
+PACK = 4
+BANK = 512
+BLOCKS = S // P
+GATHER_PIECES = ((0, 512), (512, 768), (768, 1024))
+OUT_PIECES = ((0, 256), (256, 512), (512, 768), (768, 896), (896, 1024))
+
+
+def tile_picked_mixup_gelu_p_kernel(
+    tc, x_words, x_scales, w1, w2, lam, mu, offs, pos1, out
+):
+    nc = tc.nc
+    with ExitStack() as ctx:
+        keep = ctx.enter_context(tc.tile_pool(name="keep", bufs=1))
+        psum = ctx.enter_context(tc.psum_pool(name="psum", bufs=1))
+
+        offs_sb = keep.tile([P, S // 16], U16, name="offs_sb")
+        pos_sb = keep.tile([P, S // 16], U16, name="pos_sb")
+        words_all = keep.tile([P, T], U32, name="words_all", align_bytes=64)
+        scales_all = keep.tile([P, T], U8, name="scales_all", align_bytes=64)
+        w1_raw = [keep.tile([P, PACK, H // 2], F32, name=f"w1_raw{half}") for half in range(2)]
+        w2_raw = keep.tile([P, PACK, N], F32, name="w2_raw")
+        mu_sb = keep.tile([P, S], F32, name="mu_sb")
+        lam_rows = keep.tile([P, P], F32, name="lam_rows")
+        ident = keep.tile([P, P], F32, name="ident")
+        warm = keep.tile([P, 8], F32, name="warm")
+
+        nc.vector.memset(scales_all[:].bitcast(I32), 0)
+        nc.sync.dma_start(offs_sb[:], offs)
+        nc.sync.dma_start(words_all[:].bitcast(I32), x_words[0].rearrange("p n t -> p (n t)").bitcast(I32))
+        for q in range(4):
+            nc.scalar.dma_start(
+                scales_all[32 * q : 32 * q + 4, :].bitcast(I32), x_scales[0, 4 * q : 4 * q + 4, :].bitcast(I32)
+            )
+        w1_view = w1.rearrange("(p j) c -> p j c", j=PACK)
+        for half in range(2):
+            nc.sync.dma_start(w1_raw[half][:], w1_view[:, :, half * (H // 2) : (half + 1) * (H // 2)])
+        nc.sync.dma_start(pos_sb[:], pos1)
+        nc.sync.dma_start(mu_sb[:], mu)
+        nc.sync.dma_start(w2_raw[:], w2.rearrange("(p j) c -> p j c", j=PACK))
+        nc.gpsimd.memset(lam_rows[:], 0.0)
+        nc.sync.dma_start(lam_rows[0:BLOCKS, :], lam[0].rearrange("(b p) -> b p", p=P))
+        make_identity(nc, ident[:])
+
+        nc.vector.memset(warm[:], 0.0)
+        nc.scalar.activation(warm[:], warm[:], ACT.Gelu_apprx_tanh)
+
+        x_codes = keep.tile([P, S], U32, name="x_codes", align_bytes=64)
+        x_planes = keep.tile([P, S], U8, name="x_planes", align_bytes=64)
+        nc.vector.tensor_copy(x_planes[:], scales_all[:].indirect(offs_sb[:]))
+        for half in range(2):
+            nc.vector.tensor_copy(
+                x_codes[:, half * BANK : (half + 1) * BANK],
+                words_all[:].indirect(offs_sb[:, half * (BANK // 16) : (half + 1) * (BANK // 16)]),
+            )
+
+        w1_bf = keep.tile([P, PACK, P, PACK], BF16, name="w1_bf", align_bytes=64)
+        for half in range(2):
+            nc.scalar.copy(
+                w1_bf[:, :, half * (P // 2) : (half + 1) * (P // 2), :].rearrange("p t m j -> p m j t"),
+                w1_raw[half][:].rearrange("p j (m t) -> p m j t", t=PACK),
+            )
+        w1_codes = keep.tile([P, H], U32, name="w1_codes", align_bytes=64)
+        w1_planes = keep.tile([P, H], U8, name="w1_planes", align_bytes=64)
+        for t0, t1 in ((0, 1), (1, 2), (2, 4)):
+            nc.vector.quantize_mx(
+                out=w1_codes[:, t0 * P : t1 * P].bitcast(FP8X4),
+                scales=w1_planes[:, t0 * P : t1 * P],
+                in_=w1_bf[:, t0:t1].rearrange("p t m j -> p (t m j)"),
+            )
+
+        h = [keep.tile([P, S], F32, name=f"h{t}") for t in range(PACK)]
+        for t in range(PACK):
+            for half in range(2):
+                cols = slice(half * BANK, (half + 1) * BANK)
+                acc = psum.tile([P, BANK], F32, name="acc", tag=f"mm{half}")
+                nc.tensor.matmul_mx(
+                    out=acc[:],
+                    lhsT=w1_codes[:, t * P : (t + 1) * P].bitcast(FP8X4),
+                    lhsT_scale=w1_planes[:, t * P : (t + 1) * P],
+                    rhs=x_codes[:, cols].bitcast(FP8X4),
+                    rhs_scale=x_planes[:, cols],
+                    start=True,
+                    stop=True,
+                )
+                nc.scalar.activation(h[t][:, cols], acc[:], ACT.Gelu_apprx_tanh)
+
+        lam_ps = psum.tile([P, BANK], F32, name="lam_ps", tag="back0")
+        nc.tensor.transpose(lam_ps[:, 0:P], lam_rows[:], ident[:])
+        lam_cols = keep.tile([P, BLOCKS], F32, name="lam_cols")
+        nc.scalar.copy(lam_cols[:], lam_ps[:, 0:BLOCKS])
+
+        w2_bf = keep.tile([P, N, PACK], BF16, name="w2_bf", align_bytes=64)
+        nc.scalar.copy(
+            w2_bf[:].rearrange("p (c i) j -> p c j i", i=4), w2_raw[:].rearrange("p j (c i) -> p c j i", i=4)
+        )
+        w2_codes = keep.tile([P, N], U32, name="w2_codes", align_bytes=64)
+        w2_planes = keep.tile([P, N], U8, name="w2_planes", align_bytes=64)
+        nc.vector.quantize_mx(
+            out=w2_codes[:].bitcast(FP8X4), scales=w2_planes[:], in_=w2_bf[:].rearrange("p n j -> p (n j)")
+        )
+
+        partner = {}
+
+        def gather_piece(c0, c1):
+            piece = keep.tile([P, PACK, c1 - c0], F32, name=f"partner{c0}")
+            for t in range(PACK):
+                nc.vector.tensor_tensor(
+                    piece[:, t, :], h[t][:].indirect(pos_sb[:, c0 // 16 : c1 // 16]), mu_sb[:, c0:c1], ALU.mult
+                )
+            for b in range(c0 // P, c1 // P):
+                partner[b] = piece[:, :, b * P - c0 : (b + 1) * P - c0]
+
+        own = {}
+
+        def own_share(b):
+            turned = psum.tile([P, PACK, P], F32, name="turned", tag=f"turn{b % 2}")
+            for t in range(PACK):
+                nc.tensor.transpose(turned[:, t, :], h[t][:, b * P : (b + 1) * P], ident[:])
+            scaled = keep.tile([P, PACK, P], F32, name=f"scaled{b}")
+            nc.scalar.activation(scaled[:], turned[:], ACT.Copy, scale=lam_cols[:, b : b + 1])
+            back = psum.tile([P, PACK, P], F32, name="back", tag=f"back{b % 4}")
+            for t in range(PACK):
+                nc.tensor.transpose(back[:, t, :], scaled[:, t, :], ident[:])
+            own[b] = back
+
+        z_bf = {}
+
+        def mix(c0, c1):
+            z = keep.tile([P, c1 - c0, PACK], BF16, name=f"z_bf{c0}", align_bytes=64)
+            for b in range(c0 // P, c1 // P):
+                nc.vector.tensor_tensor(
+                    z[:, b * P - c0 : (b + 1) * P - c0, :].rearrange("p (c i) t -> p c t i", i=4),
+                    partner[b].rearrange("p t (c i) -> p c t i", i=4),
+                    own[b][:].rearrange("p t (c i) -> p c t i", i=4),
+                    ALU.add,
+                )
+            z_bf[c0] = z
+
+        def second_layer(c0, c1, k):
+            width = c1 - c0
+            z_codes = keep.tile([P, width], U32, name=f"z_codes{c0}", align_bytes=64)
+            z_planes = keep.tile([P, width], U8, name=f"z_planes{c0}", align_bytes=64)
+            nc.vector.quantize_mx(
+                out=z_codes[:].bitcast(FP8X4), scales=z_planes[:], in_=z_bf[c0][:].rearrange("p c t -> p (c t)")
+            )
+            acc = psum.tile([P, BANK], F32, name="acc", tag=f"mm{k % 2}")
+            nc.tensor.matmul_mx(
+                out=acc[:, 0:width],
+                lhsT=w2_codes[:].bitcast(FP8X4),
+                lhsT_scale=w2_planes[:],
+                rhs=z_codes[:].bitcast(FP8X4),
+                rhs_scale=z_planes[:],
+                start=True,
+                stop=True,
+            )
+            result = keep.tile([P, width], F32, name=f"result{c0}")
+            nc.scalar.copy(result[:], acc[:, 0:width])
+            nc.sync.dma_start(out[:, c0:c1], result[:])
+
+        gather_piece(*GATHER_PIECES[0])
+        for b in range(4):
+            own_share(b)
+        gather_piece(*GATHER_PIECES[1])
+        mix(*OUT_PIECES[0])
+        mix(*OUT_PIECES[1])
+        second_layer(*OUT_PIECES[0], 0)
+        for b in range(4, 6):
+            own_share(b)
+        gather_piece(*GATHER_PIECES[2])
+        second_layer(*OUT_PIECES[1], 1)
+        mix(*OUT_PIECES[2])
+        for b in range(6, 8):
+            own_share(b)
+        mix(*OUT_PIECES[3])
+        second_layer(*OUT_PIECES[2], 2)
+        mix(*OUT_PIECES[4])
+        second_layer(*OUT_PIECES[3], 3)
+        second_layer(*OUT_PIECES[4], 4)

@@ -21,7 +21,7 @@ P = 128
 PACK = 4
 BANK = 512
 BLOCKS = S // P
-GATHER_PIECES = ((0, 512), (512, 768), (768, 1024))
+GATHER_PIECES = ((0, 512), (512, 1024))
 OUT_PIECES = ((0, 256), (256, 512), (512, 768), (768, 896), (896, 1024))
 
 
@@ -37,9 +37,7 @@ def tile_picked_mixup_gelu_p_kernel(
         pos_sb = keep.tile([P, S // 16], U16, name="pos_sb")
         words_all = keep.tile([P, T], U32, name="words_all", align_bytes=64)
         scales_all = keep.tile([P, T], U8, name="scales_all", align_bytes=64)
-        w1_raw = [keep.tile([P, PACK, H // 2], F32, name=f"w1_raw{half}") for half in range(2)]
-        w2_raw = keep.tile([P, PACK, N], F32, name="w2_raw")
-        mu_sb = keep.tile([P, S], F32, name="mu_sb")
+        w1_raw = [keep.tile([P, PACK, H // 2], F32, name=f"w1_raw{half}", tag=f"raw{half}") for half in range(2)]
         lam_rows = keep.tile([P, P], F32, name="lam_rows")
         ident = keep.tile([P, P], F32, name="ident")
         warm = keep.tile([P, 8], F32, name="warm")
@@ -55,23 +53,20 @@ def tile_picked_mixup_gelu_p_kernel(
         for half in range(2):
             nc.sync.dma_start(w1_raw[half][:], w1_view[:, :, half * (H // 2) : (half + 1) * (H // 2)])
         nc.sync.dma_start(pos_sb[:], pos1)
-        nc.sync.dma_start(mu_sb[:], mu)
-        nc.sync.dma_start(w2_raw[:], w2.rearrange("(p j) c -> p j c", j=PACK))
         nc.gpsimd.memset(lam_rows[:], 0.0)
         nc.sync.dma_start(lam_rows[0:BLOCKS, :], lam[0].rearrange("(b p) -> b p", p=P))
         make_identity(nc, ident[:])
 
-        nc.vector.memset(warm[:], 0.0)
-        nc.scalar.activation(warm[:], warm[:], ACT.Gelu_apprx_tanh)
+        nc.scalar.activation(warm[:], ident[:, 0:8], ACT.Gelu_apprx_tanh)
 
         x_codes = keep.tile([P, S], U32, name="x_codes", align_bytes=64)
         x_planes = keep.tile([P, S], U8, name="x_planes", align_bytes=64)
-        nc.vector.tensor_copy(x_planes[:], scales_all[:].indirect(offs_sb[:]))
-        for half in range(2):
-            nc.vector.tensor_copy(
-                x_codes[:, half * BANK : (half + 1) * BANK],
-                words_all[:].indirect(offs_sb[:, half * (BANK // 16) : (half + 1) * (BANK // 16)]),
-            )
+        for picked, window in ((x_codes, words_all), (x_planes, scales_all)):
+            for half in range(2):
+                nc.vector.tensor_copy(
+                    picked[:, half * BANK : (half + 1) * BANK],
+                    window[:].indirect(offs_sb[:, half * (BANK // 16) : (half + 1) * (BANK // 16)]),
+                )
 
         w1_bf = keep.tile([P, PACK, P, PACK], BF16, name="w1_bf", align_bytes=64)
         for half in range(2):
@@ -79,6 +74,10 @@ def tile_picked_mixup_gelu_p_kernel(
                 w1_bf[:, :, half * (P // 2) : (half + 1) * (P // 2), :].rearrange("p t m j -> p m j t"),
                 w1_raw[half][:].rearrange("p j (m t) -> p m j t", t=PACK),
             )
+        mu_sb = keep.tile([P, S], F32, name="mu_sb", tag="raw0")
+        nc.sync.dma_start(mu_sb[:], mu)
+        w2_raw = keep.tile([P, PACK, N], F32, name="w2_raw", tag="raw1")
+        nc.sync.dma_start(w2_raw[:], w2.rearrange("(p j) c -> p j c", j=PACK))
         w1_codes = keep.tile([P, H], U32, name="w1_codes", align_bytes=64)
         w1_planes = keep.tile([P, H], U8, name="w1_planes", align_bytes=64)
         for t0, t1 in ((0, 1), (1, 2), (2, 4)):
@@ -131,16 +130,21 @@ def tile_picked_mixup_gelu_p_kernel(
                 partner[b] = piece[:, :, b * P - c0 : (b + 1) * P - c0]
 
         own = {}
+        scaled_blocks = {}
+        back_tags = ("back0", "back1", "back2", "back3", "turn0", "turn1", "mm0", "mm1")
 
-        def own_share(b):
+        def turn(b):
             turned = psum.tile([P, PACK, P], F32, name="turned", tag=f"turn{b % 2}")
             for t in range(PACK):
                 nc.tensor.transpose(turned[:, t, :], h[t][:, b * P : (b + 1) * P], ident[:])
             scaled = keep.tile([P, PACK, P], F32, name=f"scaled{b}")
             nc.scalar.activation(scaled[:], turned[:], ACT.Copy, scale=lam_cols[:, b : b + 1])
-            back = psum.tile([P, PACK, P], F32, name="back", tag=f"back{b % 4}")
+            scaled_blocks[b] = scaled
+
+        def turn_back(b):
+            back = psum.tile([P, PACK, P], F32, name="back", tag=back_tags[b])
             for t in range(PACK):
-                nc.tensor.transpose(back[:, t, :], scaled[:, t, :], ident[:])
+                nc.tensor.transpose(back[:, t, :], scaled_blocks[b][:, t, :], ident[:])
             own[b] = back
 
         z_bf = {}
@@ -163,7 +167,7 @@ def tile_picked_mixup_gelu_p_kernel(
             nc.vector.quantize_mx(
                 out=z_codes[:].bitcast(FP8X4), scales=z_planes[:], in_=z_bf[c0][:].rearrange("p c t -> p (c t)")
             )
-            acc = psum.tile([P, BANK], F32, name="acc", tag=f"mm{k % 2}")
+            acc = psum.tile([P, BANK], F32, name="acc", tag=f"back{k % 4}")
             nc.tensor.matmul_mx(
                 out=acc[:, 0:width],
                 lhsT=w2_codes[:].bitcast(FP8X4),
@@ -177,22 +181,14 @@ def tile_picked_mixup_gelu_p_kernel(
             nc.scalar.copy(result[:], acc[:, 0:width])
             nc.sync.dma_start(out[:, c0:c1], result[:])
 
-        gather_piece(*GATHER_PIECES[0])
-        for b in range(4):
-            own_share(b)
-        gather_piece(*GATHER_PIECES[1])
-        mix(*OUT_PIECES[0])
-        mix(*OUT_PIECES[1])
-        second_layer(*OUT_PIECES[0], 0)
-        for b in range(4, 6):
-            own_share(b)
-        gather_piece(*GATHER_PIECES[2])
-        second_layer(*OUT_PIECES[1], 1)
-        mix(*OUT_PIECES[2])
-        for b in range(6, 8):
-            own_share(b)
-        mix(*OUT_PIECES[3])
-        second_layer(*OUT_PIECES[2], 2)
-        mix(*OUT_PIECES[4])
-        second_layer(*OUT_PIECES[3], 3)
-        second_layer(*OUT_PIECES[4], 4)
+        for piece in GATHER_PIECES:
+            gather_piece(*piece)
+        for b in range(BLOCKS):
+            turn(b)
+        for b in range(BLOCKS):
+            turn_back(b)
+        for k, piece in enumerate(OUT_PIECES):
+            mix(*piece)
+            if k > 0:
+                second_layer(*OUT_PIECES[k - 1], k - 1)
+        second_layer(*OUT_PIECES[-1], len(OUT_PIECES) - 1)

@@ -21,6 +21,8 @@ P = 128
 PACK = 4
 BANK = 512
 BLOCKS = S // P
+W1_PIECES = ((0, 128), (128, 320), (320, 512))
+X_PIECES = ((0, 512), (512, 1024))
 GATHER_PIECES = ((0, 512), (512, 1024))
 OUT_PIECES = ((0, 256), (256, 512), (512, 768), (768, 896), (896, 1024))
 
@@ -37,79 +39,96 @@ def tile_picked_mixup_gelu_p_kernel(
         pos_sb = keep.tile([P, S // 16], U16, name="pos_sb")
         words_all = keep.tile([P, T], U32, name="words_all", align_bytes=64)
         scales_all = keep.tile([P, T], U8, name="scales_all", align_bytes=64)
-        w1_raw = [keep.tile([P, PACK, H // 2], F32, name=f"w1_raw{half}", tag=f"raw{half}") for half in range(2)]
+        w1_raw = [keep.tile([P, PACK, c1 - c0], F32, name=f"w1_raw{c0}") for c0, c1 in W1_PIECES]
+        w2_raw = keep.tile([P, PACK, N], F32, name="w2_raw")
+        mu_sb = keep.tile([P, S], F32, name="mu_sb")
         lam_rows = keep.tile([P, P], F32, name="lam_rows")
         ident = keep.tile([P, P], F32, name="ident")
         warm = keep.tile([P, 8], F32, name="warm")
 
         nc.vector.memset(scales_all[:].bitcast(I32), 0)
+        w1_view = w1.rearrange("(p j) c -> p j c", j=PACK)
         nc.sync.dma_start(offs_sb[:], offs)
-        nc.sync.dma_start(words_all[:].bitcast(I32), x_words[0].rearrange("p n t -> p (n t)").bitcast(I32))
+        nc.sync.dma_start(pos_sb[:], pos1)
+        nc.sync.dma_start(w1_raw[0][:], w1_view[:, :, slice(*W1_PIECES[0])])
         for q in range(4):
-            nc.scalar.dma_start(
+            nc.sync.dma_start(
                 scales_all[32 * q : 32 * q + 4, :].bitcast(I32), x_scales[0, 4 * q : 4 * q + 4, :].bitcast(I32)
             )
-        w1_view = w1.rearrange("(p j) c -> p j c", j=PACK)
-        for half in range(2):
-            nc.sync.dma_start(w1_raw[half][:], w1_view[:, :, half * (H // 2) : (half + 1) * (H // 2)])
-        nc.sync.dma_start(pos_sb[:], pos1)
+        nc.sync.dma_start(words_all[:].bitcast(I32), x_words[0].rearrange("p n t -> p (n t)").bitcast(I32))
+        for piece in (1, 2):
+            nc.sync.dma_start(w1_raw[piece][:], w1_view[:, :, slice(*W1_PIECES[piece])])
+        nc.sync.dma_start(w2_raw[:], w2.rearrange("(p j) c -> p j c", j=PACK))
+        nc.sync.dma_start(mu_sb[:], mu)
         nc.gpsimd.memset(lam_rows[:], 0.0)
         nc.sync.dma_start(lam_rows[0:BLOCKS, :], lam[0].rearrange("(b p) -> b p", p=P))
         make_identity(nc, ident[:])
 
         nc.scalar.activation(warm[:], ident[:, 0:8], ACT.Gelu_apprx_tanh)
 
-        x_codes = keep.tile([P, S], U32, name="x_codes", align_bytes=64)
         x_planes = keep.tile([P, S], U8, name="x_planes", align_bytes=64)
-        for picked, window in ((x_codes, words_all), (x_planes, scales_all)):
-            for half in range(2):
-                nc.vector.tensor_copy(
-                    picked[:, half * BANK : (half + 1) * BANK],
-                    window[:].indirect(offs_sb[:, half * (BANK // 16) : (half + 1) * (BANK // 16)]),
-                )
-
-        w1_bf = keep.tile([P, PACK, P, PACK], BF16, name="w1_bf", align_bytes=64)
         for half in range(2):
-            nc.scalar.copy(
-                w1_bf[:, :, half * (P // 2) : (half + 1) * (P // 2), :].rearrange("p t m j -> p m j t"),
-                w1_raw[half][:].rearrange("p j (m t) -> p m j t", t=PACK),
+            nc.vector.tensor_copy(
+                x_planes[:, half * BANK : (half + 1) * BANK],
+                scales_all[:].indirect(offs_sb[:, half * (BANK // 16) : (half + 1) * (BANK // 16)]),
             )
-        mu_sb = keep.tile([P, S], F32, name="mu_sb", tag="raw0")
-        nc.sync.dma_start(mu_sb[:], mu)
-        w2_raw = keep.tile([P, PACK, N], F32, name="w2_raw", tag="raw1")
-        nc.sync.dma_start(w2_raw[:], w2.rearrange("(p j) c -> p j c", j=PACK))
+        x_codes = {}
+
+        def gather_words(c0, c1, tag):
+            picked = keep.tile([P, c1 - c0], U32, name=f"x_codes{c0}", tag=tag, align_bytes=64)
+            nc.vector.tensor_copy(picked[:], words_all[:].indirect(offs_sb[:, c0 // 16 : c1 // 16]))
+            x_codes[c0] = picked
+
+        gather_words(*X_PIECES[0], "x_first")
+        gather_words(*X_PIECES[1], "x_second")
+
+        w1_first = keep.tile([P, P, PACK], BF16, name="w1_first", tag="first", align_bytes=64)
+        w1_rest = keep.tile([P, PACK - 1, P, PACK], BF16, name="w1_rest", align_bytes=64)
+        for raw, (c0, c1) in zip(w1_raw, W1_PIECES):
+            by_tile = raw[:].rearrange("p j (m t) -> p m j t", t=PACK)
+            nc.scalar.copy(w1_first[:, c0 // PACK : c1 // PACK, :], by_tile[:, :, :, 0])
+            nc.scalar.copy(
+                w1_rest[:, :, c0 // PACK : c1 // PACK, :].rearrange("p t m j -> p m j t"), by_tile[:, :, :, 1:PACK]
+            )
         w1_codes = keep.tile([P, H], U32, name="w1_codes", align_bytes=64)
         w1_planes = keep.tile([P, H], U8, name="w1_planes", align_bytes=64)
-        for t0, t1 in ((0, 1), (1, 2), (2, 4)):
+        nc.vector.quantize_mx(
+            out=w1_codes[:, 0:P].bitcast(FP8X4),
+            scales=w1_planes[:, 0:P],
+            in_=w1_first[:].rearrange("p m j -> p (m j)"),
+        )
+        for t0, t1 in ((1, 2), (2, 4)):
             nc.vector.quantize_mx(
                 out=w1_codes[:, t0 * P : t1 * P].bitcast(FP8X4),
                 scales=w1_planes[:, t0 * P : t1 * P],
-                in_=w1_bf[:, t0:t1].rearrange("p t m j -> p (t m j)"),
+                in_=w1_rest[:, t0 - 1 : t1 - 1].rearrange("p t m j -> p (t m j)"),
             )
 
         h = [keep.tile([P, S], F32, name=f"h{t}") for t in range(PACK)]
         for t in range(PACK):
             for half in range(2):
                 cols = slice(half * BANK, (half + 1) * BANK)
-                acc = psum.tile([P, BANK], F32, name="acc", tag=f"mm{half}")
-                nc.tensor.matmul_mx(
-                    out=acc[:],
-                    lhsT=w1_codes[:, t * P : (t + 1) * P].bitcast(FP8X4),
-                    lhsT_scale=w1_planes[:, t * P : (t + 1) * P],
-                    rhs=x_codes[:, cols].bitcast(FP8X4),
-                    rhs_scale=x_planes[:, cols],
-                    start=True,
-                    stop=True,
-                )
+                acc = psum.tile([P, BANK], F32, name="acc", tag=f"bank{6 + half}")
+                for c0, c1 in X_PIECES:
+                    if c0 // BANK == half:
+                        nc.tensor.matmul_mx(
+                            out=acc[:, c0 - half * BANK : c1 - half * BANK],
+                            lhsT=w1_codes[:, t * P : (t + 1) * P].bitcast(FP8X4),
+                            lhsT_scale=w1_planes[:, t * P : (t + 1) * P],
+                            rhs=x_codes[c0][:].bitcast(FP8X4),
+                            rhs_scale=x_planes[:, c0:c1],
+                            start=True,
+                            stop=True,
+                        )
                 nc.scalar.activation(h[t][:, cols], acc[:], ACT.Gelu_apprx_tanh)
 
-        lam_ps = psum.tile([P, BANK], F32, name="lam_ps", tag="back0")
+        lam_ps = psum.tile([P, BANK], F32, name="lam_ps", tag="bank6")
         nc.tensor.transpose(lam_ps[:, 0:P], lam_rows[:], ident[:])
         lam_cols = keep.tile([P, BLOCKS], F32, name="lam_cols")
         nc.scalar.copy(lam_cols[:], lam_ps[:, 0:BLOCKS])
 
         w2_bf = keep.tile([P, N, PACK], BF16, name="w2_bf", align_bytes=64)
-        nc.scalar.copy(
+        nc.vector.tensor_copy(
             w2_bf[:].rearrange("p (c i) j -> p c j i", i=4), w2_raw[:].rearrange("p j (c i) -> p c j i", i=4)
         )
         w2_codes = keep.tile([P, N], U32, name="w2_codes", align_bytes=64)
@@ -131,10 +150,9 @@ def tile_picked_mixup_gelu_p_kernel(
 
         own = {}
         scaled_blocks = {}
-        back_tags = ("back0", "back1", "back2", "back3", "turn0", "turn1", "mm0", "mm1")
 
         def turn(b):
-            turned = psum.tile([P, PACK, P], F32, name="turned", tag=f"turn{b % 2}")
+            turned = psum.tile([P, PACK, P], F32, name="turned", tag=f"bank{b}")
             for t in range(PACK):
                 nc.tensor.transpose(turned[:, t, :], h[t][:, b * P : (b + 1) * P], ident[:])
             scaled = keep.tile([P, PACK, P], F32, name=f"scaled{b}")
@@ -142,7 +160,7 @@ def tile_picked_mixup_gelu_p_kernel(
             scaled_blocks[b] = scaled
 
         def turn_back(b):
-            back = psum.tile([P, PACK, P], F32, name="back", tag=back_tags[b])
+            back = psum.tile([P, PACK, P], F32, name="back", tag=f"bank{b}")
             for t in range(PACK):
                 nc.tensor.transpose(back[:, t, :], scaled_blocks[b][:, t, :], ident[:])
             own[b] = back
@@ -167,7 +185,7 @@ def tile_picked_mixup_gelu_p_kernel(
             nc.vector.quantize_mx(
                 out=z_codes[:].bitcast(FP8X4), scales=z_planes[:], in_=z_bf[c0][:].rearrange("p c t -> p (c t)")
             )
-            acc = psum.tile([P, BANK], F32, name="acc", tag=f"back{k % 4}")
+            acc = psum.tile([P, BANK], F32, name="acc", tag=f"bank{k}")
             nc.tensor.matmul_mx(
                 out=acc[:, 0:width],
                 lhsT=w2_codes[:].bitcast(FP8X4),
@@ -179,7 +197,8 @@ def tile_picked_mixup_gelu_p_kernel(
             )
             result = keep.tile([P, width], F32, name=f"result{c0}")
             nc.scalar.copy(result[:], acc[:, 0:width])
-            nc.sync.dma_start(out[:, c0:c1], result[:])
+            queue = nc.scalar if c1 == S else nc.sync
+            queue.dma_start(out[:, c0:c1], result[:])
 
         for piece in GATHER_PIECES:
             gather_piece(*piece)

@@ -1,7 +1,6 @@
 from contextlib import ExitStack
 
 import concourse.mybir as mybir
-from concourse.masks import make_identity
 
 K, T, S, H, N = 512, 2048, 1024, 512, 128
 FLOPS = 2 * K * H * S + 2 * H * N * S
@@ -21,9 +20,9 @@ P = 128
 PACK = 4
 BANK = 512
 BLOCKS = S // P
-W1_PIECES = ((0, 128), (128, 320), (320, 512))
-X_PIECES = ((0, 512), (512, 1024))
-GATHER_PIECES = ((0, 512), (512, 1024))
+TILES = H // P
+W1_PIECES = ((0, 1), (1, 2), (2, 4))
+X_PIECES = ((0, 512), (512, 768), (768, 1024))
 OUT_PIECES = ((0, 256), (256, 512), (512, 768), (768, 896), (896, 1024))
 
 
@@ -37,98 +36,105 @@ def tile_picked_mixup_gelu_p_kernel(
 
         offs_sb = keep.tile([P, S // 16], U16, name="offs_sb")
         pos_sb = keep.tile([P, S // 16], U16, name="pos_sb")
-        words_all = keep.tile([P, T], U32, name="words_all", align_bytes=64)
-        scales_all = keep.tile([P, T], U8, name="scales_all", align_bytes=64)
-        w1_raw = [keep.tile([P, PACK, c1 - c0], F32, name=f"w1_raw{c0}") for c0, c1 in W1_PIECES]
+        words_all = keep.tile([P, T], U32, name="words_all", tag="words", align_bytes=64)
+        scales_all = keep.tile([P, T], U8, name="scales_all", tag="scales", align_bytes=64)
+        w1_raw = [
+            keep.tile([P, PACK, (t1 - t0) * P], F32, name=f"w1_raw{t0}", tag=f"raw{t0}", align_bytes=64) for t0, t1 in W1_PIECES
+        ]
         w2_raw = keep.tile([P, PACK, N], F32, name="w2_raw")
-        mu_sb = keep.tile([P, S], F32, name="mu_sb")
-        lam_rows = keep.tile([P, P], F32, name="lam_rows")
+        share_rows = keep.tile([P, P], F32, name="share_rows")
         ident = keep.tile([P, P], F32, name="ident")
-        warm = keep.tile([P, 8], F32, name="warm")
+        ones = keep.tile([P, P], F32, name="ones")
+        base = keep.tile([P, 1], F32, name="base")
+        counts = keep.tile([P, P], F32, name="counts", align_bytes=64)
+        row_number = keep.tile([P, 32], F32, name="row_number", align_bytes=64)
+        warm = keep.tile([P, 1], F32, name="warm")
 
         nc.vector.memset(scales_all[:].bitcast(I32), 0)
+        nc.gpsimd.memset(share_rows[:], 0.0)
+        nc.vector.memset(ones[:], 1.0)
+        nc.scalar.activation(warm[:], ones[:, 0:1], ACT.Gelu_apprx_tanh)
         w1_view = w1.rearrange("(p j) c -> p j c", j=PACK)
+        nc.sync.dma_start(share_rows[0:BLOCKS, :], lam[0].rearrange("(b p) -> b p", p=P))
+        nc.sync.dma_start(share_rows[BLOCKS : 2 * BLOCKS, :], mu[0].rearrange("(b p) -> b p", p=P))
         nc.sync.dma_start(offs_sb[:], offs)
-        nc.sync.dma_start(pos_sb[:], pos1)
-        nc.sync.dma_start(w1_raw[0][:], w1_view[:, :, slice(*W1_PIECES[0])])
         for q in range(4):
             nc.sync.dma_start(
                 scales_all[32 * q : 32 * q + 4, :].bitcast(I32), x_scales[0, 4 * q : 4 * q + 4, :].bitcast(I32)
             )
         nc.sync.dma_start(words_all[:].bitcast(I32), x_words[0].rearrange("p n t -> p (n t)").bitcast(I32))
-        for piece in (1, 2):
-            nc.sync.dma_start(w1_raw[piece][:], w1_view[:, :, slice(*W1_PIECES[piece])])
+        nc.sync.dma_start(w1_raw[0][:], w1_view[:, :, 0:P])
+        nc.sync.dma_start(pos_sb[:], pos1)
         nc.sync.dma_start(w2_raw[:], w2.rearrange("(p j) c -> p j c", j=PACK))
-        nc.sync.dma_start(mu_sb[:], mu)
-        nc.gpsimd.memset(lam_rows[:], 0.0)
-        nc.sync.dma_start(lam_rows[0:BLOCKS, :], lam[0].rearrange("(b p) -> b p", p=P))
-        make_identity(nc, ident[:])
+        nc.sync.dma_start(w1_raw[1][:], w1_view[:, :, P : 2 * P])
+        nc.sync.dma_start(w1_raw[2][:], w1_view[:, :, 2 * P : H])
+        for q in range(4):
+            nc.gpsimd.memset(base[32 * q : 32 * q + 32, :], 32.0 * q)
+        nc.vector.tensor_tensor_scan(counts[:], ones[:], ones[:], base[:], ALU.mult, ALU.add)
+        nc.vector.transpose(row_number[:], counts[:, 0:32])
+        nc.vector.tensor_scalar(ident[:], counts[:], base[:], row_number[:, 0:1], ALU.subtract, ALU.is_equal)
 
-        nc.scalar.activation(warm[:], ident[:, 0:8], ACT.Gelu_apprx_tanh)
 
-        x_planes = keep.tile([P, S], U8, name="x_planes", align_bytes=64)
+        shares = psum.tile([P, BANK], F32, name="shares", tag="bank4")
+        nc.tensor.transpose(shares[:, 0:P], share_rows[:], ident[:])
+        own_cols = keep.tile([P, BLOCKS], F32, name="own_cols")
+        inv_cols = keep.tile([P, BLOCKS], F32, name="inv_cols")
+        ratio_cols = keep.tile([P, BLOCKS], F32, name="ratio_cols")
+        nc.vector.tensor_scalar(own_cols[:], shares[:, 0:BLOCKS], 2.0**-60, 2.0**-100, ALU.add, ALU.add)
+        nc.vector.reciprocal(inv_cols[:], own_cols[:])
+        nc.vector.tensor_tensor(ratio_cols[:], shares[:, BLOCKS : 2 * BLOCKS], inv_cols[:], ALU.mult)
+        ratio = []
+
+        def spread_ratio(half, bank, tag):
+            spread = psum.tile([P, PACK, P], F32, name="spread", tag=f"bank{bank}")
+            for i in range(PACK):
+                b = half * PACK + i
+                nc.tensor.transpose(spread[:, i, :], ratio_cols[:, b : b + 1].to_broadcast([P, P]), ident[:])
+            ratio.append(keep.tile([P, BANK], F32, name=f"ratio{half}", tag=tag, align_bytes=64))
+            nc.scalar.copy(ratio[half][:], spread[:].rearrange("p i s -> p (i s)"))
+
+        spread_ratio(0, 0, "ratio0")
+        spread_ratio(1, 1, "ratio1")
+
+        x_planes = []
         for half in range(2):
+            x_planes.append(keep.tile([P, BANK], U8, name=f"x_planes{half}", tag=f"planes{half}", align_bytes=64))
             nc.vector.tensor_copy(
-                x_planes[:, half * BANK : (half + 1) * BANK],
+                x_planes[half][:],
                 scales_all[:].indirect(offs_sb[:, half * (BANK // 16) : (half + 1) * (BANK // 16)]),
             )
-        x_codes = {}
 
-        def gather_words(c0, c1, tag):
-            picked = keep.tile([P, c1 - c0], U32, name=f"x_codes{c0}", tag=tag, align_bytes=64)
-            nc.vector.tensor_copy(picked[:], words_all[:].indirect(offs_sb[:, c0 // 16 : c1 // 16]))
-            x_codes[c0] = picked
-
-        gather_words(*X_PIECES[0], "x_first")
-        gather_words(*X_PIECES[1], "x_second")
-
-        w1_first = keep.tile([P, P, PACK], BF16, name="w1_first", tag="first", align_bytes=64)
-        w1_rest = keep.tile([P, PACK - 1, P, PACK], BF16, name="w1_rest", align_bytes=64)
-        for raw, (c0, c1) in zip(w1_raw, W1_PIECES):
-            by_tile = raw[:].rearrange("p j (m t) -> p m j t", t=PACK)
-            nc.scalar.copy(w1_first[:, c0 // PACK : c1 // PACK, :], by_tile[:, :, :, 0])
-            nc.scalar.copy(
-                w1_rest[:, :, c0 // PACK : c1 // PACK, :].rearrange("p t m j -> p m j t"), by_tile[:, :, :, 1:PACK]
-            )
         w1_codes = keep.tile([P, H], U32, name="w1_codes", align_bytes=64)
-        w1_planes = keep.tile([P, H], U8, name="w1_planes", align_bytes=64)
-        nc.vector.quantize_mx(
-            out=w1_codes[:, 0:P].bitcast(FP8X4),
-            scales=w1_planes[:, 0:P],
-            in_=w1_first[:].rearrange("p m j -> p (m j)"),
-        )
-        for t0, t1 in ((1, 2), (2, 4)):
+        w1_planes = {}
+
+        def quantise_w1(piece, copy, rounded_tag, plane_tag):
+            t0, t1 = W1_PIECES[piece]
+            rounded = keep.tile([P, (t1 - t0) * P, PACK], BF16, name=f"w1_bf{t0}", tag=rounded_tag, align_bytes=64)
+            plane = keep.tile([P, (t1 - t0) * P], U8, name=f"w1_planes{t0}", tag=plane_tag, align_bytes=64)
+            for t in range(t0, t1):
+                w1_planes[t] = plane[:, (t - t0) * P : (t - t0 + 1) * P]
+            copy(
+                rounded[:].rearrange("p (c i) j -> p c j i", i=4),
+                w1_raw[piece][:].rearrange("p j (c i) -> p c j i", i=4),
+            )
             nc.vector.quantize_mx(
                 out=w1_codes[:, t0 * P : t1 * P].bitcast(FP8X4),
-                scales=w1_planes[:, t0 * P : t1 * P],
-                in_=w1_rest[:, t0 - 1 : t1 - 1].rearrange("p t m j -> p (t m j)"),
+                scales=plane[:],
+                in_=rounded[:].rearrange("p c j -> p (c j)"),
             )
 
-        h = [keep.tile([P, S], F32, name=f"h{t}") for t in range(PACK)]
-        for t in range(PACK):
-            for half in range(2):
-                cols = slice(half * BANK, (half + 1) * BANK)
-                acc = psum.tile([P, BANK], F32, name="acc", tag=f"bank{6 + half}")
-                for c0, c1 in X_PIECES:
-                    if c0 // BANK == half:
-                        nc.tensor.matmul_mx(
-                            out=acc[:, c0 - half * BANK : c1 - half * BANK],
-                            lhsT=w1_codes[:, t * P : (t + 1) * P].bitcast(FP8X4),
-                            lhsT_scale=w1_planes[:, t * P : (t + 1) * P],
-                            rhs=x_codes[c0][:].bitcast(FP8X4),
-                            rhs_scale=x_planes[:, c0:c1],
-                            start=True,
-                            stop=True,
-                        )
-                nc.scalar.activation(h[t][:, cols], acc[:], ACT.Gelu_apprx_tanh)
-
-        lam_ps = psum.tile([P, BANK], F32, name="lam_ps", tag="bank6")
-        nc.tensor.transpose(lam_ps[:, 0:P], lam_rows[:], ident[:])
-        lam_cols = keep.tile([P, BLOCKS], F32, name="lam_cols")
-        nc.scalar.copy(lam_cols[:], lam_ps[:, 0:BLOCKS])
-
+        quantise_w1(0, nc.scalar.copy, "rounded0", "scales")
+        x_codes = [
+            keep.tile([P, BANK], U32, name="x_codes0", align_bytes=64),
+            keep.tile([P, BANK], U32, name="x_codes1", tag="raw0", align_bytes=64),
+        ]
+        for c0, c1 in X_PIECES:
+            nc.vector.tensor_copy(
+                x_codes[c0 // BANK][:, c0 % BANK : c0 % BANK + c1 - c0],
+                words_all[:].indirect(offs_sb[:, c0 // 16 : c1 // 16]),
+            )
         w2_bf = keep.tile([P, N, PACK], BF16, name="w2_bf", align_bytes=64)
-        nc.vector.tensor_copy(
+        nc.scalar.copy(
             w2_bf[:].rearrange("p (c i) j -> p c j i", i=4), w2_raw[:].rearrange("p j (c i) -> p c j i", i=4)
         )
         w2_codes = keep.tile([P, N], U32, name="w2_codes", align_bytes=64)
@@ -137,77 +143,182 @@ def tile_picked_mixup_gelu_p_kernel(
             out=w2_codes[:].bitcast(FP8X4), scales=w2_planes[:], in_=w2_bf[:].rearrange("p n j -> p (n j)")
         )
 
-        partner = {}
+        quantise_w1(1, nc.scalar.copy, "rounded1", "w1_planes1")
+        quantise_w1(2, nc.vector.tensor_copy, "rounded2", "w1_planes2")
 
-        def gather_piece(c0, c1):
-            piece = keep.tile([P, PACK, c1 - c0], F32, name=f"partner{c0}")
-            for t in range(PACK):
-                nc.vector.tensor_tensor(
-                    piece[:, t, :], h[t][:].indirect(pos_sb[:, c0 // 16 : c1 // 16]), mu_sb[:, c0:c1], ALU.mult
-                )
-            for b in range(c0 // P, c1 // P):
-                partner[b] = piece[:, :, b * P - c0 : (b + 1) * P - c0]
+        h = [
+            keep.tile([P, S], F32, name=f"h{t}", tag=("raw1" if t == 0 else f"h{t}"), align_bytes=64)
+            for t in range(TILES)
+        ]
 
-        own = {}
-        scaled_blocks = {}
-
-        def turn(b):
-            turned = psum.tile([P, PACK, P], F32, name="turned", tag=f"bank{b}")
-            for t in range(PACK):
-                nc.tensor.transpose(turned[:, t, :], h[t][:, b * P : (b + 1) * P], ident[:])
-            scaled = keep.tile([P, PACK, P], F32, name=f"scaled{b}")
-            nc.scalar.activation(scaled[:], turned[:], ACT.Copy, scale=lam_cols[:, b : b + 1])
-            scaled_blocks[b] = scaled
-
-        def turn_back(b):
-            back = psum.tile([P, PACK, P], F32, name="back", tag=f"bank{b}")
-            for t in range(PACK):
-                nc.tensor.transpose(back[:, t, :], scaled_blocks[b][:, t, :], ident[:])
-            own[b] = back
-
-        z_bf = {}
-
-        def mix(c0, c1):
-            z = keep.tile([P, c1 - c0, PACK], BF16, name=f"z_bf{c0}", align_bytes=64)
-            for b in range(c0 // P, c1 // P):
-                nc.vector.tensor_tensor(
-                    z[:, b * P - c0 : (b + 1) * P - c0, :].rearrange("p (c i) t -> p c t i", i=4),
-                    partner[b].rearrange("p t (c i) -> p c t i", i=4),
-                    own[b][:].rearrange("p t (c i) -> p c t i", i=4),
-                    ALU.add,
-                )
-            z_bf[c0] = z
-
-        def second_layer(c0, c1, k):
-            width = c1 - c0
-            z_codes = keep.tile([P, width], U32, name=f"z_codes{c0}", align_bytes=64)
-            z_planes = keep.tile([P, width], U8, name=f"z_planes{c0}", align_bytes=64)
-            nc.vector.quantize_mx(
-                out=z_codes[:].bitcast(FP8X4), scales=z_planes[:], in_=z_bf[c0][:].rearrange("p c t -> p (c t)")
-            )
-            acc = psum.tile([P, BANK], F32, name="acc", tag=f"bank{k}")
+        def first_layer(t, c0, c1, bank):
+            acc = psum.tile([P, BANK], F32, name="acc", tag=f"bank{bank}")
             nc.tensor.matmul_mx(
-                out=acc[:, 0:width],
-                lhsT=w2_codes[:].bitcast(FP8X4),
-                lhsT_scale=w2_planes[:],
-                rhs=z_codes[:].bitcast(FP8X4),
-                rhs_scale=z_planes[:],
+                out=acc[:, 0 : c1 - c0],
+                lhsT=w1_codes[:, t * P : (t + 1) * P].bitcast(FP8X4),
+                lhsT_scale=w1_planes[t],
+                rhs=x_codes[c0 // BANK][:, c0 % BANK : c0 % BANK + c1 - c0].bitcast(FP8X4),
+                rhs_scale=x_planes[c0 // BANK][:, c0 % BANK : c0 % BANK + c1 - c0],
                 start=True,
                 stop=True,
             )
-            result = keep.tile([P, width], F32, name=f"result{c0}")
-            nc.scalar.copy(result[:], acc[:, 0:width])
+            nc.scalar.activation(h[t][:, c0:c1], acc[:, 0 : c1 - c0], ACT.Gelu_apprx_tanh)
+
+        for i, (c0, c1) in enumerate(X_PIECES):
+            first_layer(0, c0, c1, 5 + i)
+        for t in range(1, TILES):
+            for half in range(2):
+                first_layer(t, half * BANK, (half + 1) * BANK, 5 + (2 * t - 2 + half) % 3)
+
+        partner = {}
+
+        def partner_tile(tiles, b0, b1, tag):
+            held = keep.tile([P, len(tiles), (b1 - b0) * P], F32, name=f"partner{b0}", tag=tag, align_bytes=64)
+            for i, t in enumerate(tiles):
+                for b in range(b0, b1):
+                    partner[t, b] = (held[:, i, :], (b - b0) * P)
+
+        def gather(t, c0, c1):
+            row, start = partner[t, c0 // P]
+            nc.vector.tensor_tensor(
+                row[:, start : start + c1 - c0],
+                h[t][:].indirect(pos_sb[:, c0 // 16 : c1 // 16]),
+                ratio[c0 // BANK][:, c0 % BANK : c0 % BANK + c1 - c0],
+                ALU.mult,
+            )
+
+        sums = {}
+
+        def group(b, t):
+            if b < BLOCKS - 1:
+                return 0, TILES, b
+            return (0, TILES - 1, b) if t < TILES - 1 else (TILES - 1, TILES, 2)
+
+        def turn_own(b, t):
+            t0, t1, bank = group(b, t)
+            if t == t0:
+                sums[b, t0] = psum.tile([P, H], F32, name="sums", tag=f"bank{bank}")
+            nc.tensor.matmul(
+                sums[b, t0][:, t * P : (t + 1) * P],
+                h[t][:, b * P : (b + 1) * P],
+                ident[:],
+                start=(t == t0),
+                stop=False,
+                is_transpose=True,
+            )
+
+        def turn_partner(b, t):
+            row, start = partner[t, b]
+            t0, t1, bank = group(b, t)
+            nc.tensor.matmul(
+                sums[b, t0][:, t * P : (t + 1) * P],
+                row[:, start : start + P],
+                ident[:],
+                start=False,
+                stop=(t == t1 - 1),
+                is_transpose=True,
+            )
+
+        z_rows = {}
+
+        def scale(b, t0=0, t1=TILES):
+            if t0 == 0:
+                z_rows[b] = keep.tile([P, 2, P, 2], BF16, name=f"z_rows{b}", tag=f"rows{b}", align_bytes=64)
+            nc.scalar.activation(
+                z_rows[b][:, :, 32 * t0 : 32 * t1, :],
+                sums[b, t0][:, t0 * P : t1 * P].rearrange("s (p u e) -> s u p e", u=2, e=2),
+                ACT.Copy,
+                scale=own_cols[:, b : b + 1],
+            )
+
+        z_bf = {c0: keep.tile([P, c1 - c0, PACK], BF16, name=f"z_bf{c0}", align_bytes=64) for c0, c1 in OUT_PIECES}
+
+        def turn_back(b, copy):
+            back = psum.tile([P, PACK, P], F32, name="back", tag=f"bank{b}")
+            words = z_rows[b][:].rearrange("s u p e -> s (u p e)").bitcast(F32)
+            for u in range(2):
+                nc.tensor.transpose(back[:, u, :], words[:, u * P : (u + 1) * P], ident[:])
+            c0 = max(c for c, _ in OUT_PIECES if c <= b * P)
+            pairs = z_bf[c0][:].rearrange("p s t -> p (s t)").bitcast(F32).rearrange("p (s u) -> p s u", u=2)
+            copy(pairs[:, b * P - c0 : (b + 1) * P - c0, :], back[:, 0:2, :].rearrange("p u s -> p s u"))
+
+        def second_product(k, acc):
+            c0, c1 = OUT_PIECES[k]
+            z_codes = keep.tile([P, c1 - c0], U32, name=f"z_codes{c0}", align_bytes=64)
+            z_planes = z_planes_all[:, c0:c1]
+            nc.vector.quantize_mx(
+                out=z_codes[:].bitcast(FP8X4), scales=z_planes, in_=z_bf[c0][:].rearrange("p c t -> p (c t)")
+            )
+            nc.tensor.matmul_mx(
+                out=acc,
+                lhsT=w2_codes[:].bitcast(FP8X4),
+                lhsT_scale=w2_planes[:],
+                rhs=z_codes[:].bitcast(FP8X4),
+                rhs_scale=z_planes,
+                start=True,
+                stop=True,
+            )
+
+        def store(pieces, bank, copy):
+            c0, c1 = OUT_PIECES[pieces[0]][0], OUT_PIECES[pieces[-1]][1]
+            acc = psum.tile([P, BANK], F32, name="acc", tag=f"bank{bank}")
+            for k in pieces:
+                second_product(k, acc[:, OUT_PIECES[k][0] - c0 : OUT_PIECES[k][1] - c0])
+            result = keep.tile([P, c1 - c0], F32, name=f"result{c0}")
+            copy(result[:], acc[:, 0 : c1 - c0])
             queue = nc.scalar if c1 == S else nc.sync
             queue.dma_start(out[:, c0:c1], result[:])
 
-        for piece in GATHER_PIECES:
-            gather_piece(*piece)
-        for b in range(BLOCKS):
-            turn(b)
-        for b in range(BLOCKS):
-            turn_back(b)
-        for k, piece in enumerate(OUT_PIECES):
-            mix(*piece)
-            if k > 0:
-                second_layer(*OUT_PIECES[k - 1], k - 1)
-        second_layer(*OUT_PIECES[-1], len(OUT_PIECES) - 1)
+        def mix(b):
+            for t in range(TILES):
+                turn_partner(b, t)
+            scale(b)
+
+        partner_tile(range(TILES), 0, 4, "raw2")
+        for t in range(TILES - 1):
+            gather(t, 0, BANK)
+            for b in range(5):
+                turn_own(b, t)
+            for b in range(4):
+                turn_partner(b, t)
+        for b in range(5):
+            turn_own(b, TILES - 1)
+        for b0, b1 in ((0, 1), (1, 2), (2, 4)):
+            gather(TILES - 1, b0 * P, b1 * P)
+            for b in range(b0, b1):
+                turn_partner(b, TILES - 1)
+                scale(b)
+        for b in range(5, BLOCKS):
+            for t in range(TILES if b < BLOCKS - 1 else TILES - 1):
+                turn_own(b, t)
+        partner_tile(range(TILES), 4, 7, "ratio0")
+        for b0, b1 in ((4, 6), (6, 7)):
+            for t in range(TILES):
+                gather(t, b0 * P, b1 * P)
+        turn_back(0, nc.scalar.copy)
+        turn_back(1, nc.scalar.copy)
+        turn_back(2, nc.scalar.copy)
+        turn_own(7, TILES - 1)
+        mix(4)
+        mix(5)
+        turn_back(3, nc.scalar.copy)
+        partner_tile(range(TILES - 1), 7, 8, "rows3")
+        for t in range(TILES - 1):
+            gather(t, 7 * P, S)
+        mix(6)
+        turn_back(4, nc.scalar.copy)
+        turn_back(5, nc.scalar.copy)
+        partner_tile([TILES - 1], 7, 8, "rows5")
+        gather(TILES - 1, 7 * P, S)
+        for t in range(TILES - 1):
+            turn_partner(7, t)
+        scale(7, 0, TILES - 1)
+        turn_partner(7, TILES - 1)
+        scale(7, TILES - 1, TILES)
+        turn_back(6, nc.scalar.copy)
+        z_planes_all = keep.tile([P, S], U8, name="z_planes_all", tag="ratio1", align_bytes=64)
+        store([0], 0, nc.scalar.copy)
+        store([1], 1, nc.scalar.copy)
+        turn_back(7, nc.vector.tensor_copy)
+        store([2, 3], 2, nc.vector.tensor_copy)
+        store([4], 3, nc.scalar.copy)

@@ -21,6 +21,7 @@ PACK = 4
 BANK = 512
 BLOCKS = S // P
 TILES = H // P
+RUN = S // P
 W1_PIECES = ((0, 1), (1, 2), (2, 4))
 X_PIECES = ((0, 512), (512, 768), (768, 1024))
 OUT_PIECES = ((0, 256), (256, 512), (512, 768), (768, 896), (896, 1024))
@@ -43,6 +44,8 @@ def tile_picked_mixup_gelu_p_kernel(
         ]
         w2_raw = keep.tile([P, PACK, N], F32, name="w2_raw")
         share_rows = keep.tile([P, P], F32, name="share_rows")
+        lam_runs = keep.tile([P, RUN], F32, name="lam_runs")
+        mu_runs = keep.tile([P, RUN], F32, name="mu_runs")
         ident = keep.tile([P, P], F32, name="ident")
         ones = keep.tile([P, P], F32, name="ones")
         base = keep.tile([P, 1], F32, name="base")
@@ -55,8 +58,8 @@ def tile_picked_mixup_gelu_p_kernel(
         nc.vector.memset(ones[:], 1.0)
         nc.scalar.activation(warm[:], ones[:, 0:1], ACT.Gelu_apprx_tanh)
         w1_view = w1.rearrange("(p j) c -> p j c", j=PACK)
-        nc.sync.dma_start(share_rows[0:BLOCKS, :], lam[0].rearrange("(b p) -> b p", p=P))
-        nc.sync.dma_start(share_rows[BLOCKS : 2 * BLOCKS, :], mu[0].rearrange("(b p) -> b p", p=P))
+        nc.sync.dma_start(lam_runs[:], lam[0].rearrange("(p c) -> p c", c=RUN))
+        nc.sync.dma_start(mu_runs[:], mu[0].rearrange("(p c) -> p c", c=RUN))
         nc.sync.dma_start(offs_sb[:], offs)
         for q in range(4):
             nc.sync.dma_start(
@@ -64,6 +67,7 @@ def tile_picked_mixup_gelu_p_kernel(
             )
         nc.sync.dma_start(words_all[:].bitcast(I32), x_words[0].rearrange("p n t -> p (n t)").bitcast(I32))
         nc.sync.dma_start(w1_raw[0][:], w1_view[:, :, 0:P])
+        nc.sync.dma_start(share_rows[0:BLOCKS, :], lam[0].rearrange("(b p) -> b p", p=P))
         nc.sync.dma_start(pos_sb[:], pos1)
         nc.sync.dma_start(w2_raw[:], w2.rearrange("(p j) c -> p j c", j=PACK))
         nc.sync.dma_start(w1_raw[1][:], w1_view[:, :, P : 2 * P])
@@ -75,26 +79,25 @@ def tile_picked_mixup_gelu_p_kernel(
         nc.vector.tensor_scalar(ident[:], counts[:], base[:], row_number[:, 0:1], ALU.subtract, ALU.is_equal)
 
 
-        shares = psum.tile([P, BANK], F32, name="shares", tag="bank4")
-        nc.tensor.transpose(shares[:, 0:P], share_rows[:], ident[:])
-        own_cols = keep.tile([P, BLOCKS], F32, name="own_cols")
-        inv_cols = keep.tile([P, BLOCKS], F32, name="inv_cols")
-        ratio_cols = keep.tile([P, BLOCKS], F32, name="ratio_cols")
-        nc.vector.tensor_scalar(own_cols[:], shares[:, 0:BLOCKS], 2.0**-60, 2.0**-100, ALU.add, ALU.add)
-        nc.vector.reciprocal(inv_cols[:], own_cols[:])
-        nc.vector.tensor_tensor(ratio_cols[:], shares[:, BLOCKS : 2 * BLOCKS], inv_cols[:], ALU.mult)
-        ratio = []
-
-        def spread_ratio(half, bank, tag):
-            spread = psum.tile([P, PACK, P], F32, name="spread", tag=f"bank{bank}")
+        own_runs = keep.tile([P, RUN], F32, name="own_runs")
+        inv_runs = keep.tile([P, RUN], F32, name="inv_runs")
+        ratio_runs = keep.tile([P, RUN], F32, name="ratio_runs")
+        nc.vector.tensor_scalar(own_runs[:], lam_runs[:], 2.0**-60, 2.0**-100, ALU.add, ALU.add)
+        nc.vector.reciprocal(inv_runs[:], own_runs[:])
+        nc.vector.tensor_tensor(ratio_runs[:], mu_runs[:], inv_runs[:], ALU.mult)
+        ratio = [
+            keep.tile([P, BANK], F32, name=f"ratio{half}", tag=f"ratio{half}", align_bytes=64) for half in range(2)
+        ]
+        for quad in range(2):
+            spread = psum.tile([P, PACK, P], F32, name="spread", tag=f"bank{quad}")
             for i in range(PACK):
-                b = half * PACK + i
-                nc.tensor.transpose(spread[:, i, :], ratio_cols[:, b : b + 1].to_broadcast([P, P]), ident[:])
-            ratio.append(keep.tile([P, BANK], F32, name=f"ratio{half}", tag=tag, align_bytes=64))
-            nc.scalar.copy(ratio[half][:], spread[:].rearrange("p i s -> p (i s)"))
-
-        spread_ratio(0, 0, "ratio0")
-        spread_ratio(1, 1, "ratio1")
+                c = quad * PACK + i
+                nc.tensor.transpose(spread[:, i, :], ratio_runs[:, c : c + 1].to_broadcast([P, P]), ident[:])
+            for half in range(2):
+                nc.scalar.copy(
+                    ratio[half][:].rearrange("q (n c) -> q n c", c=RUN)[:, :, quad * PACK : (quad + 1) * PACK],
+                    spread[:, :, half * 64 : (half + 1) * 64].rearrange("q i n -> q n i"),
+                )
 
         x_planes = []
         for half in range(2):
@@ -113,17 +116,27 @@ def tile_picked_mixup_gelu_p_kernel(
             plane = keep.tile([P, (t1 - t0) * P], U8, name=f"w1_planes{t0}", tag=plane_tag, align_bytes=64)
             for t in range(t0, t1):
                 w1_planes[t] = plane[:, (t - t0) * P : (t - t0 + 1) * P]
-            copy(
-                rounded[:].rearrange("p (c i) j -> p c j i", i=4),
-                w1_raw[piece][:].rearrange("p j (c i) -> p c j i", i=4),
-            )
-            nc.vector.quantize_mx(
-                out=w1_codes[:, t0 * P : t1 * P].bitcast(FP8X4),
-                scales=plane[:],
-                in_=rounded[:].rearrange("p c j -> p (c j)"),
-            )
+            for t in range(t0, t1):
+                cols = slice((t - t0) * P, (t - t0 + 1) * P)
+                copy(
+                    rounded[:, cols, :].rearrange("p (c i) j -> p c j i", i=4),
+                    w1_raw[piece][:, :, cols].rearrange("p j (c i) -> p c j i", i=4),
+                )
+            for t in range(t0, t1):
+                cols = slice((t - t0) * P, (t - t0 + 1) * P)
+                nc.vector.quantize_mx(
+                    out=w1_codes[:, t * P : (t + 1) * P].bitcast(FP8X4),
+                    scales=w1_planes[t],
+                    in_=rounded[:, cols, :].rearrange("p c j -> p (c j)"),
+                )
 
         quantise_w1(0, nc.scalar.copy, "rounded0", "scales")
+        shares = psum.tile([P, BANK], F32, name="shares", tag="bank3")
+        nc.tensor.transpose(shares[:, 0:P], share_rows[:], ident[:])
+        nudged = keep.tile([P, BLOCKS], F32, name="nudged")
+        own_cols = keep.tile([P, BLOCKS], F32, name="own_cols")
+        nc.scalar.activation(nudged[:], shares[:, 0:BLOCKS], ACT.Copy, bias=2.0**-60)
+        nc.scalar.activation(own_cols[:], nudged[:], ACT.Copy, bias=2.0**-100)
         x_codes = [
             keep.tile([P, BANK], U32, name="x_codes0", align_bytes=64),
             keep.tile([P, BANK], U32, name="x_codes1", tag="raw0", align_bytes=64),
@@ -165,10 +178,10 @@ def tile_picked_mixup_gelu_p_kernel(
             nc.scalar.activation(h[t][:, c0:c1], acc[:, 0 : c1 - c0], ACT.Gelu_apprx_tanh)
 
         for i, (c0, c1) in enumerate(X_PIECES):
-            first_layer(0, c0, c1, 5 + i)
+            first_layer(0, c0, c1, 4 + i)
         for t in range(1, TILES):
             for half in range(2):
-                first_layer(t, half * BANK, (half + 1) * BANK, 5 + (2 * t - 2 + half) % 3)
+                first_layer(t, half * BANK, (half + 1) * BANK, 4 + (2 * t + 1 + half) % 4)
 
         partner = {}
 
@@ -189,10 +202,15 @@ def tile_picked_mixup_gelu_p_kernel(
 
         sums = {}
 
+        def bank_of(b):
+            return b if b < 4 else 4 + (b - 3) % 4
+
         def group(b, t):
+            if b < 4:
+                return (0, 2, b) if t < 2 else (2, TILES, b)
             if b < BLOCKS - 1:
-                return 0, TILES, b
-            return (0, TILES - 1, b) if t < TILES - 1 else (TILES - 1, TILES, 2)
+                return 0, TILES, bank_of(b)
+            return (0, TILES - 1, bank_of(b)) if t < TILES - 1 else (TILES - 1, TILES, 2)
 
         def turn_own(b, t):
             t0, t1, bank = group(b, t)
@@ -234,7 +252,7 @@ def tile_picked_mixup_gelu_p_kernel(
         z_bf = {c0: keep.tile([P, c1 - c0, PACK], BF16, name=f"z_bf{c0}", align_bytes=64) for c0, c1 in OUT_PIECES}
 
         def turn_back(b, copy):
-            back = psum.tile([P, PACK, P], F32, name="back", tag=f"bank{b}")
+            back = psum.tile([P, PACK, P], F32, name="back", tag=f"bank{bank_of(b)}")
             words = z_rows[b][:].rearrange("s u p e -> s (u p e)").bitcast(F32)
             for u in range(2):
                 nc.tensor.transpose(back[:, u, :], words[:, u * P : (u + 1) * P], ident[:])
@@ -275,20 +293,24 @@ def tile_picked_mixup_gelu_p_kernel(
             scale(b)
 
         partner_tile(range(TILES), 0, 4, "raw2")
-        for t in range(TILES - 1):
+        for t in range(2):
             gather(t, 0, BANK)
-            for b in range(5):
+            for b in range(4):
                 turn_own(b, t)
             for b in range(4):
                 turn_partner(b, t)
-        for b in range(5):
-            turn_own(b, TILES - 1)
-        for b0, b1 in ((0, 1), (1, 2), (2, 4)):
+        gather(2, 0, BANK)
+        for b in range(4):
+            scale(b, 0, 2)
+            turn_own(b, 2)
+            turn_partner(b, 2)
+            turn_own(b, 3)
+        for b0, b1 in ((0, 2), (2, 4)):
             gather(TILES - 1, b0 * P, b1 * P)
             for b in range(b0, b1):
                 turn_partner(b, TILES - 1)
-                scale(b)
-        for b in range(5, BLOCKS):
+                scale(b, 2, TILES)
+        for b in range(4, BLOCKS):
             for t in range(TILES if b < BLOCKS - 1 else TILES - 1):
                 turn_own(b, t)
         partner_tile(range(TILES), 4, 7, "ratio0")
@@ -318,7 +340,7 @@ def tile_picked_mixup_gelu_p_kernel(
         turn_back(6, nc.scalar.copy)
         z_planes_all = keep.tile([P, S], U8, name="z_planes_all", tag="ratio1", align_bytes=64)
         store([0], 0, nc.scalar.copy)
-        store([1], 1, nc.scalar.copy)
         turn_back(7, nc.vector.tensor_copy)
+        store([1], bank_of(6), nc.scalar.copy)
         store([2, 3], 2, nc.vector.tensor_copy)
         store([4], 3, nc.scalar.copy)

@@ -22,9 +22,11 @@ BANK = 512
 BLOCKS = S // P
 TILES = H // P
 RUN = S // P
-W1_PIECES = ((0, 1), (1, 2), (2, 4))
-X_PIECES = ((0, 512), (512, 768), (768, 1024))
-OUT_PIECES = ((0, 256), (256, 512), (512, 768), (768, 896), (896, 1024))
+W1_PIECES = ((0, 64), (64, 96), (96, 128))
+FIRST_PIECES = ((0, 256), (256, 512), (512, 768), (768, 1024))
+OUT_PIECES = ((0, 512), (512, 768), (768, 896), (896, 1024))
+TURNED = 7
+TAIL = S - TURNED * P
 
 
 def tile_picked_mixup_gelu_p_kernel(
@@ -37,15 +39,15 @@ def tile_picked_mixup_gelu_p_kernel(
 
         offs_sb = keep.tile([P, S // 16], U16, name="offs_sb")
         pos_sb = keep.tile([P, S // 16], U16, name="pos_sb")
-        words_all = keep.tile([P, T], U32, name="words_all", tag="words", align_bytes=64)
-        scales_all = keep.tile([P, T], U8, name="scales_all", tag="scales", align_bytes=64)
-        w1_raw = [
-            keep.tile([P, PACK, (t1 - t0) * P], F32, name=f"w1_raw{t0}", tag=f"raw{t0}", align_bytes=64) for t0, t1 in W1_PIECES
-        ]
+        words_all = keep.tile([P, T], U32, name="words_all", align_bytes=64)
+        scales_all = keep.tile([P, T], U8, name="scales_all", align_bytes=64)
+        w1_raw = [keep.tile([P, PACK, PACK * (m1 - m0)], F32, name=f"w1_raw{m0}", align_bytes=64) for m0, m1 in W1_PIECES]
         w2_raw = keep.tile([P, PACK, N], F32, name="w2_raw")
         share_rows = keep.tile([P, P], F32, name="share_rows")
         lam_runs = keep.tile([P, RUN], F32, name="lam_runs")
         mu_runs = keep.tile([P, RUN], F32, name="mu_runs")
+        lam_tail = keep.tile([P, TAIL], F32, name="lam_tail")
+        mu_tail = keep.tile([P, TAIL], F32, name="mu_tail")
         ident = keep.tile([P, P], F32, name="ident")
         ones = keep.tile([P, P], F32, name="ones")
         base = keep.tile([P, 1], F32, name="base")
@@ -53,7 +55,7 @@ def tile_picked_mixup_gelu_p_kernel(
         row_number = keep.tile([P, 32], F32, name="row_number", align_bytes=64)
         warm = keep.tile([P, 1], F32, name="warm")
 
-        nc.vector.memset(scales_all[:].bitcast(I32), 0)
+        nc.gpsimd.memset(scales_all[:].bitcast(I32), 0)
         nc.gpsimd.memset(share_rows[:], 0.0)
         nc.vector.memset(ones[:], 1.0)
         nc.scalar.activation(warm[:], ones[:, 0:1], ACT.Gelu_apprx_tanh)
@@ -66,18 +68,18 @@ def tile_picked_mixup_gelu_p_kernel(
                 scales_all[32 * q : 32 * q + 4, :].bitcast(I32), x_scales[0, 4 * q : 4 * q + 4, :].bitcast(I32)
             )
         nc.sync.dma_start(words_all[:].bitcast(I32), x_words[0].rearrange("p n t -> p (n t)").bitcast(I32))
-        nc.sync.dma_start(w1_raw[0][:], w1_view[:, :, 0:P])
         nc.sync.dma_start(share_rows[0:BLOCKS, :], lam[0].rearrange("(b p) -> b p", p=P))
+        for i, (m0, m1) in enumerate(W1_PIECES):
+            nc.sync.dma_start(w1_raw[i][:], w1_view[:, :, PACK * m0 : PACK * m1])
         nc.sync.dma_start(pos_sb[:], pos1)
         nc.sync.dma_start(w2_raw[:], w2.rearrange("(p j) c -> p j c", j=PACK))
-        nc.sync.dma_start(w1_raw[1][:], w1_view[:, :, P : 2 * P])
-        nc.sync.dma_start(w1_raw[2][:], w1_view[:, :, 2 * P : H])
+        nc.sync.dma_start(lam_tail[:], lam[:, TURNED * P : S])
+        nc.sync.dma_start(mu_tail[:], mu[:, TURNED * P : S])
         for q in range(4):
-            nc.gpsimd.memset(base[32 * q : 32 * q + 32, :], 32.0 * q)
+            nc.vector.memset(base[32 * q : 32 * q + 32, :], 32.0 * q)
         nc.vector.tensor_tensor_scan(counts[:], ones[:], ones[:], base[:], ALU.mult, ALU.add)
         nc.vector.transpose(row_number[:], counts[:, 0:32])
         nc.vector.tensor_scalar(ident[:], counts[:], base[:], row_number[:, 0:1], ALU.subtract, ALU.is_equal)
-
 
         own_runs = keep.tile([P, RUN], F32, name="own_runs")
         inv_runs = keep.tile([P, RUN], F32, name="inv_runs")
@@ -85,8 +87,9 @@ def tile_picked_mixup_gelu_p_kernel(
         nc.vector.tensor_scalar(own_runs[:], lam_runs[:], 2.0**-60, 2.0**-100, ALU.add, ALU.add)
         nc.vector.reciprocal(inv_runs[:], own_runs[:])
         nc.vector.tensor_tensor(ratio_runs[:], mu_runs[:], inv_runs[:], ALU.mult)
+        widths = (BANK, TURNED * P - BANK)
         ratio = [
-            keep.tile([P, BANK], F32, name=f"ratio{half}", tag=f"ratio{half}", align_bytes=64) for half in range(2)
+            keep.tile([P, widths[half]], F32, name=f"ratio{half}", tag=f"ratio{half}", align_bytes=64) for half in range(2)
         ]
         for quad in range(2):
             spread = psum.tile([P, PACK, P], F32, name="spread", tag=f"bank{quad}")
@@ -96,80 +99,69 @@ def tile_picked_mixup_gelu_p_kernel(
             for half in range(2):
                 nc.scalar.copy(
                     ratio[half][:].rearrange("q (n c) -> q n c", c=RUN)[:, :, quad * PACK : (quad + 1) * PACK],
-                    spread[:, :, half * 64 : (half + 1) * 64].rearrange("q i n -> q n i"),
+                    spread[:, :, half * 64 : half * 64 + widths[half] // RUN].rearrange("q i n -> q n i"),
                 )
-
-        x_planes = []
-        for half in range(2):
-            x_planes.append(keep.tile([P, BANK], U8, name=f"x_planes{half}", tag=f"planes{half}", align_bytes=64))
-            nc.vector.tensor_copy(
-                x_planes[half][:],
-                scales_all[:].indirect(offs_sb[:, half * (BANK // 16) : (half + 1) * (BANK // 16)]),
-            )
-
-        w1_codes = keep.tile([P, H], U32, name="w1_codes", align_bytes=64)
-        w1_planes = {}
-
-        def quantise_w1(piece, copy, rounded_tag, plane_tag):
-            t0, t1 = W1_PIECES[piece]
-            rounded = keep.tile([P, (t1 - t0) * P, PACK], BF16, name=f"w1_bf{t0}", tag=rounded_tag, align_bytes=64)
-            plane = keep.tile([P, (t1 - t0) * P], U8, name=f"w1_planes{t0}", tag=plane_tag, align_bytes=64)
-            for t in range(t0, t1):
-                w1_planes[t] = plane[:, (t - t0) * P : (t - t0 + 1) * P]
-            for t in range(t0, t1):
-                cols = slice((t - t0) * P, (t - t0 + 1) * P)
-                copy(
-                    rounded[:, cols, :].rearrange("p (c i) j -> p c j i", i=4),
-                    w1_raw[piece][:, :, cols].rearrange("p j (c i) -> p c j i", i=4),
-                )
-            for t in range(t0, t1):
-                cols = slice((t - t0) * P, (t - t0 + 1) * P)
-                nc.vector.quantize_mx(
-                    out=w1_codes[:, t * P : (t + 1) * P].bitcast(FP8X4),
-                    scales=w1_planes[t],
-                    in_=rounded[:, cols, :].rearrange("p c j -> p (c j)"),
-                )
-
-        quantise_w1(0, nc.scalar.copy, "rounded0", "scales")
         shares = psum.tile([P, BANK], F32, name="shares", tag="bank3")
         nc.tensor.transpose(shares[:, 0:P], share_rows[:], ident[:])
         nudged = keep.tile([P, BLOCKS], F32, name="nudged")
         own_cols = keep.tile([P, BLOCKS], F32, name="own_cols")
         nc.scalar.activation(nudged[:], shares[:, 0:BLOCKS], ACT.Copy, bias=2.0**-60)
         nc.scalar.activation(own_cols[:], nudged[:], ACT.Copy, bias=2.0**-100)
-        x_codes = [
-            keep.tile([P, BANK], U32, name="x_codes0", align_bytes=64),
-            keep.tile([P, BANK], U32, name="x_codes1", tag="raw0", align_bytes=64),
-        ]
-        for c0, c1 in X_PIECES:
-            nc.vector.tensor_copy(
-                x_codes[c0 // BANK][:, c0 % BANK : c0 % BANK + c1 - c0],
-                words_all[:].indirect(offs_sb[:, c0 // 16 : c1 // 16]),
+
+        x_planes = [keep.tile([P, BANK], U8, name=f"x_planes{half}", align_bytes=64) for half in range(2)]
+        x_codes = [keep.tile([P, BANK], U32, name=f"x_codes{half}", align_bytes=64) for half in range(2)]
+        for table, picked in ((scales_all, x_planes), (words_all, x_codes)):
+            for half in range(2):
+                nc.vector.tensor_copy(
+                    picked[half][:], table[:].indirect(offs_sb[:, half * (BANK // 16) : (half + 1) * (BANK // 16)])
+                )
+
+        w1_codes = keep.tile([P, H], U32, name="w1_codes", align_bytes=64)
+        w1_planes = keep.tile([P, H], U8, name="w1_planes", align_bytes=64)
+        w1_bf = {}
+
+        def round_w1(u, piece, copy):
+            m0, m1 = W1_PIECES[piece]
+            if piece == 0:
+                w1_bf[u] = keep.tile([P, 2, P, PACK], BF16, name=f"w1_bf{u}", tag="w1_bf", align_bytes=64)
+            copy(
+                w1_bf[u][:, :, m0:m1, :].rearrange("p e m j -> p m j e"),
+                w1_raw[piece][:].rearrange("p j (m t) -> p m j t", t=PACK)[:, :, :, 2 * u : 2 * u + 2],
             )
+
+        def quantise_w1(t):
+            nc.vector.quantize_mx(
+                out=w1_codes[:, t * P : (t + 1) * P].bitcast(FP8X4),
+                scales=w1_planes[:, t * P : (t + 1) * P],
+                in_=w1_bf[t // 2][:, t % 2, :, :].rearrange("p m j -> p (m j)"),
+            )
+
+        for piece in range(len(W1_PIECES)):
+            round_w1(0, piece, nc.scalar.copy)
+        quantise_w1(0)
+        quantise_w1(1)
         w2_bf = keep.tile([P, N, PACK], BF16, name="w2_bf", align_bytes=64)
-        nc.scalar.copy(
+        nc.vector.tensor_copy(
             w2_bf[:].rearrange("p (c i) j -> p c j i", i=4), w2_raw[:].rearrange("p j (c i) -> p c j i", i=4)
         )
+        for piece in range(len(W1_PIECES)):
+            round_w1(1, piece, nc.vector.tensor_copy)
         w2_codes = keep.tile([P, N], U32, name="w2_codes", align_bytes=64)
         w2_planes = keep.tile([P, N], U8, name="w2_planes", align_bytes=64)
         nc.vector.quantize_mx(
             out=w2_codes[:].bitcast(FP8X4), scales=w2_planes[:], in_=w2_bf[:].rearrange("p n j -> p (n j)")
         )
+        quantise_w1(2)
+        quantise_w1(3)
 
-        quantise_w1(1, nc.scalar.copy, "rounded1", "w1_planes1")
-        quantise_w1(2, nc.vector.tensor_copy, "rounded2", "w1_planes2")
-
-        h = [
-            keep.tile([P, S], F32, name=f"h{t}", tag=("raw1" if t == 0 else f"h{t}"), align_bytes=64)
-            for t in range(TILES)
-        ]
+        h = [keep.tile([P, S], F32, name=f"h{t}", align_bytes=64) for t in range(TILES)]
 
         def first_layer(t, c0, c1, bank):
             acc = psum.tile([P, BANK], F32, name="acc", tag=f"bank{bank}")
             nc.tensor.matmul_mx(
                 out=acc[:, 0 : c1 - c0],
                 lhsT=w1_codes[:, t * P : (t + 1) * P].bitcast(FP8X4),
-                lhsT_scale=w1_planes[t],
+                lhsT_scale=w1_planes[:, t * P : (t + 1) * P],
                 rhs=x_codes[c0 // BANK][:, c0 % BANK : c0 % BANK + c1 - c0].bitcast(FP8X4),
                 rhs_scale=x_planes[c0 // BANK][:, c0 % BANK : c0 % BANK + c1 - c0],
                 start=True,
@@ -177,45 +169,41 @@ def tile_picked_mixup_gelu_p_kernel(
             )
             nc.scalar.activation(h[t][:, c0:c1], acc[:, 0 : c1 - c0], ACT.Gelu_apprx_tanh)
 
-        for i, (c0, c1) in enumerate(X_PIECES):
-            first_layer(0, c0, c1, 4 + i)
+        for i, (c0, c1) in enumerate(FIRST_PIECES):
+            first_layer(0, c0, c1, (6, 7, 4, 5)[i])
         for t in range(1, TILES):
             for half in range(2):
-                first_layer(t, half * BANK, (half + 1) * BANK, 4 + (2 * t + 1 + half) % 4)
+                first_layer(t, half * BANK, (half + 1) * BANK, 4 + (2 * t + half) % 4)
 
         partner = {}
 
-        def partner_tile(tiles, b0, b1, tag):
-            held = keep.tile([P, len(tiles), (b1 - b0) * P], F32, name=f"partner{b0}", tag=tag, align_bytes=64)
-            for i, t in enumerate(tiles):
+        def partner_tile(b0, b1, tag):
+            held = keep.tile([P, TILES, (b1 - b0) * P], F32, name=f"partner{b0}", tag=tag, align_bytes=64)
+            for t in range(TILES):
                 for b in range(b0, b1):
-                    partner[t, b] = (held[:, i, :], (b - b0) * P)
+                    partner[t, b] = (held[:, t, :], (b - b0) * P)
+            return held
 
-        def gather(t, c0, c1):
+        def gather(t, c0, c1, factor):
             row, start = partner[t, c0 // P]
             nc.vector.tensor_tensor(
-                row[:, start : start + c1 - c0],
-                h[t][:].indirect(pos_sb[:, c0 // 16 : c1 // 16]),
-                ratio[c0 // BANK][:, c0 % BANK : c0 % BANK + c1 - c0],
-                ALU.mult,
+                row[:, start : start + c1 - c0], h[t][:].indirect(pos_sb[:, c0 // 16 : c1 // 16]), factor, ALU.mult
             )
+
+        def gather_turned(t, c0, c1):
+            gather(t, c0, c1, ratio[c0 // BANK][:, c0 % BANK : c0 % BANK + c1 - c0])
 
         sums = {}
 
-        def bank_of(b):
-            return b if b < 4 else 4 + (b - 3) % 4
-
         def group(b, t):
             if b < 4:
-                return (0, 2, b) if t < 2 else (2, TILES, b)
-            if b < BLOCKS - 1:
-                return 0, TILES, bank_of(b)
-            return (0, TILES - 1, bank_of(b)) if t < TILES - 1 else (TILES - 1, TILES, 2)
+                return (0, 2) if t < 2 else (2, TILES)
+            return 0, TILES
 
         def turn_own(b, t):
-            t0, t1, bank = group(b, t)
+            t0, t1 = group(b, t)
             if t == t0:
-                sums[b, t0] = psum.tile([P, H], F32, name="sums", tag=f"bank{bank}")
+                sums[b, t0] = psum.tile([P, H], F32, name="sums", tag=f"bank{b}")
             nc.tensor.matmul(
                 sums[b, t0][:, t * P : (t + 1) * P],
                 h[t][:, b * P : (b + 1) * P],
@@ -227,7 +215,7 @@ def tile_picked_mixup_gelu_p_kernel(
 
         def turn_partner(b, t):
             row, start = partner[t, b]
-            t0, t1, bank = group(b, t)
+            t0, t1 = group(b, t)
             nc.tensor.matmul(
                 sums[b, t0][:, t * P : (t + 1) * P],
                 row[:, start : start + P],
@@ -243,48 +231,48 @@ def tile_picked_mixup_gelu_p_kernel(
             if t0 == 0:
                 z_rows[b] = keep.tile([P, 2, P, 2], BF16, name=f"z_rows{b}", tag=f"rows{b}", align_bytes=64)
             nc.scalar.activation(
-                z_rows[b][:, :, 32 * t0 : 32 * t1, :],
-                sums[b, t0][:, t0 * P : t1 * P].rearrange("s (p u e) -> s u p e", u=2, e=2),
+                z_rows[b][:, t0 // 2 : t1 // 2, :, :],
+                sums[b, t0][:, t0 * P : t1 * P].rearrange("s (u e p) -> s u p e", e=2, p=P),
                 ACT.Copy,
                 scale=own_cols[:, b : b + 1],
             )
 
         z_bf = {c0: keep.tile([P, c1 - c0, PACK], BF16, name=f"z_bf{c0}", align_bytes=64) for c0, c1 in OUT_PIECES}
 
-        def turn_back(b, copy):
-            back = psum.tile([P, PACK, P], F32, name="back", tag=f"bank{bank_of(b)}")
+        def turn_back(b):
+            back = psum.tile([P, PACK, P], F32, name="back", tag=f"bank{b}")
             words = z_rows[b][:].rearrange("s u p e -> s (u p e)").bitcast(F32)
             for u in range(2):
                 nc.tensor.transpose(back[:, u, :], words[:, u * P : (u + 1) * P], ident[:])
             c0 = max(c for c, _ in OUT_PIECES if c <= b * P)
             pairs = z_bf[c0][:].rearrange("p s t -> p (s t)").bitcast(F32).rearrange("p (s u) -> p s u", u=2)
-            copy(pairs[:, b * P - c0 : (b + 1) * P - c0, :], back[:, 0:2, :].rearrange("p u s -> p s u"))
+            nc.scalar.copy(pairs[:, b * P - c0 : (b + 1) * P - c0, :], back[:, 0:2, :].rearrange("p u s -> p s u"))
 
-        def second_product(k, acc):
+        z_mx = {}
+
+        def quantise_z(k, tag):
             c0, c1 = OUT_PIECES[k]
-            z_codes = keep.tile([P, c1 - c0], U32, name=f"z_codes{c0}", align_bytes=64)
-            z_planes = z_planes_all[:, c0:c1]
+            z_codes = keep.tile([P, c1 - c0], U32, name=f"z_codes{c0}", tag=tag, align_bytes=64)
+            z_planes = keep.tile([P, c1 - c0], U8, name=f"z_planes{c0}", align_bytes=64)
             nc.vector.quantize_mx(
-                out=z_codes[:].bitcast(FP8X4), scales=z_planes, in_=z_bf[c0][:].rearrange("p c t -> p (c t)")
+                out=z_codes[:].bitcast(FP8X4), scales=z_planes[:], in_=z_bf[c0][:].rearrange("p c t -> p (c t)")
             )
+            z_mx[k] = (z_codes, z_planes)
+
+        def store(k, bank, copy, queue):
+            c0, c1 = OUT_PIECES[k]
+            acc = psum.tile([P, BANK], F32, name="acc", tag=f"bank{bank}")
             nc.tensor.matmul_mx(
-                out=acc,
+                out=acc[:, 0 : c1 - c0],
                 lhsT=w2_codes[:].bitcast(FP8X4),
                 lhsT_scale=w2_planes[:],
-                rhs=z_codes[:].bitcast(FP8X4),
-                rhs_scale=z_planes,
+                rhs=z_mx[k][0][:].bitcast(FP8X4),
+                rhs_scale=z_mx[k][1][:],
                 start=True,
                 stop=True,
             )
-
-        def store(pieces, bank, copy):
-            c0, c1 = OUT_PIECES[pieces[0]][0], OUT_PIECES[pieces[-1]][1]
-            acc = psum.tile([P, BANK], F32, name="acc", tag=f"bank{bank}")
-            for k in pieces:
-                second_product(k, acc[:, OUT_PIECES[k][0] - c0 : OUT_PIECES[k][1] - c0])
             result = keep.tile([P, c1 - c0], F32, name=f"result{c0}")
             copy(result[:], acc[:, 0 : c1 - c0])
-            queue = nc.scalar if c1 == S else nc.sync
             queue.dma_start(out[:, c0:c1], result[:])
 
         def mix(b):
@@ -292,55 +280,58 @@ def tile_picked_mixup_gelu_p_kernel(
                 turn_partner(b, t)
             scale(b)
 
-        partner_tile(range(TILES), 0, 4, "raw2")
+        partner_tile(0, 4, "partner0")
         for t in range(2):
-            gather(t, 0, BANK)
+            gather_turned(t, 0, BANK)
             for b in range(4):
                 turn_own(b, t)
             for b in range(4):
                 turn_partner(b, t)
-        gather(2, 0, BANK)
+        gather_turned(2, 0, BANK)
         for b in range(4):
             scale(b, 0, 2)
             turn_own(b, 2)
             turn_partner(b, 2)
             turn_own(b, 3)
         for b0, b1 in ((0, 2), (2, 4)):
-            gather(TILES - 1, b0 * P, b1 * P)
+            gather_turned(TILES - 1, b0 * P, b1 * P)
             for b in range(b0, b1):
                 turn_partner(b, TILES - 1)
                 scale(b, 2, TILES)
-        for b in range(4, BLOCKS):
-            for t in range(TILES if b < BLOCKS - 1 else TILES - 1):
+        for b in range(4, TURNED):
+            for t in range(TILES):
                 turn_own(b, t)
-        partner_tile(range(TILES), 4, 7, "ratio0")
+        partner_tile(4, TURNED, "ratio0")
         for b0, b1 in ((4, 6), (6, 7)):
             for t in range(TILES):
-                gather(t, b0 * P, b1 * P)
-        turn_back(0, nc.scalar.copy)
-        turn_back(1, nc.scalar.copy)
-        turn_back(2, nc.scalar.copy)
-        turn_own(7, TILES - 1)
+                gather_turned(t, b0 * P, b1 * P)
+        turn_back(0)
+        turn_back(1)
+        own_tail = keep.tile([P, TILES, TAIL], F32, name="own_tail", tag="rows1", align_bytes=64)
+        for t in range(TILES):
+            nc.vector.tensor_tensor(own_tail[:, t, :], h[t][:, TURNED * P : S], lam_tail[:], ALU.mult)
+        turn_back(2)
         mix(4)
         mix(5)
-        turn_back(3, nc.scalar.copy)
-        partner_tile(range(TILES - 1), 7, 8, "rows3")
-        for t in range(TILES - 1):
-            gather(t, 7 * P, S)
+        turn_back(3)
+        quantise_z(0, "z_codes0")
+        partner_tail = partner_tile(TURNED, BLOCKS, "rows3")
+        for t in range(TILES):
+            gather(t, TURNED * P, S, mu_tail[:])
         mix(6)
-        turn_back(4, nc.scalar.copy)
-        turn_back(5, nc.scalar.copy)
-        partner_tile([TILES - 1], 7, 8, "rows5")
-        gather(TILES - 1, 7 * P, S)
-        for t in range(TILES - 1):
-            turn_partner(7, t)
-        scale(7, 0, TILES - 1)
-        turn_partner(7, TILES - 1)
-        scale(7, TILES - 1, TILES)
-        turn_back(6, nc.scalar.copy)
-        z_planes_all = keep.tile([P, S], U8, name="z_planes_all", tag="ratio1", align_bytes=64)
-        store([0], 0, nc.scalar.copy)
-        turn_back(7, nc.vector.tensor_copy)
-        store([1], bank_of(6), nc.scalar.copy)
-        store([2, 3], 2, nc.vector.tensor_copy)
-        store([4], 3, nc.scalar.copy)
+        turn_back(4)
+        turn_back(5)
+        turn_back(6)
+        quantise_z(1, "z_codes1")
+        nc.vector.tensor_tensor(
+            z_bf[TURNED * P][:].rearrange("p (c i) t -> p c t i", i=4),
+            own_tail[:].rearrange("p t (c i) -> p c t i", i=4),
+            partner_tail[:].rearrange("p t (c i) -> p c t i", i=4),
+            ALU.add,
+        )
+        quantise_z(2, "z_codes2")
+        quantise_z(3, "rows6")
+        store(0, 5, nc.scalar.copy, nc.sync)
+        store(1, 0, nc.scalar.copy, nc.sync)
+        store(2, 1, nc.vector.tensor_copy, nc.sync)
+        store(3, 2, nc.scalar.copy, nc.scalar)

@@ -24,7 +24,9 @@ TILES = H // P
 RUN = S // P
 W1_PIECES = ((0, 64), (64, 96), (96, 128))
 FIRST_PIECES = ((0, 256), (256, 512), (512, 768), (768, 1024))
-OUT_PIECES = ((0, 512), (512, 768), (768, 896), (896, 1024))
+GATHERS = (((0, 896),), ((0, 512), (512, 896)), ((0, 896),), ((0, 256), (256, 512), (512, 768), (768, 896)))
+PAIRS = BLOCKS // 2
+WIDE = 2 * P
 TURNED = 7
 TAIL = S - TURNED * P
 
@@ -87,20 +89,16 @@ def tile_picked_mixup_gelu_p_kernel(
         nc.vector.tensor_scalar(own_runs[:], lam_runs[:], 2.0**-60, 2.0**-100, ALU.add, ALU.add)
         nc.vector.reciprocal(inv_runs[:], own_runs[:])
         nc.vector.tensor_tensor(ratio_runs[:], mu_runs[:], inv_runs[:], ALU.mult)
-        widths = (BANK, TURNED * P - BANK)
-        ratio = [
-            keep.tile([P, widths[half]], F32, name=f"ratio{half}", tag=f"ratio{half}", align_bytes=64) for half in range(2)
-        ]
+        ratio = keep.tile([P, TURNED * P], F32, name="ratio", align_bytes=64)
         for quad in range(2):
             spread = psum.tile([P, PACK, P], F32, name="spread", tag=f"bank{quad}")
             for i in range(PACK):
                 c = quad * PACK + i
                 nc.tensor.transpose(spread[:, i, :], ratio_runs[:, c : c + 1].to_broadcast([P, P]), ident[:])
-            for half in range(2):
-                nc.scalar.copy(
-                    ratio[half][:].rearrange("q (n c) -> q n c", c=RUN)[:, :, quad * PACK : (quad + 1) * PACK],
-                    spread[:, :, half * 64 : half * 64 + widths[half] // RUN].rearrange("q i n -> q n i"),
-                )
+            nc.scalar.copy(
+                ratio[:].rearrange("q (n c) -> q n c", c=RUN)[:, :, quad * PACK : (quad + 1) * PACK],
+                spread[:, :, 0 : TURNED * P // RUN].rearrange("q i n -> q n i"),
+            )
         shares = psum.tile([P, BANK], F32, name="shares", tag="bank3")
         nc.tensor.transpose(shares[:, 0:P], share_rows[:], ident[:])
         nudged = keep.tile([P, BLOCKS], F32, name="nudged")
@@ -108,13 +106,10 @@ def tile_picked_mixup_gelu_p_kernel(
         nc.scalar.activation(nudged[:], shares[:, 0:BLOCKS], ACT.Copy, bias=2.0**-60)
         nc.scalar.activation(own_cols[:], nudged[:], ACT.Copy, bias=2.0**-100)
 
-        x_planes = [keep.tile([P, BANK], U8, name=f"x_planes{half}", align_bytes=64) for half in range(2)]
-        x_codes = [keep.tile([P, BANK], U32, name=f"x_codes{half}", align_bytes=64) for half in range(2)]
-        for table, picked in ((scales_all, x_planes), (words_all, x_codes)):
-            for half in range(2):
-                nc.vector.tensor_copy(
-                    picked[half][:], table[:].indirect(offs_sb[:, half * (BANK // 16) : (half + 1) * (BANK // 16)])
-                )
+        x_planes = keep.tile([P, S], U8, name="x_planes", align_bytes=64)
+        x_codes = keep.tile([P, S], U32, name="x_codes", align_bytes=64)
+        nc.vector.tensor_copy(x_planes[:], scales_all[:].indirect(offs_sb[:]))
+        nc.vector.tensor_copy(x_codes[:], words_all[:].indirect(offs_sb[:]))
 
         w1_codes = keep.tile([P, H], U32, name="w1_codes", align_bytes=64)
         w1_planes = keep.tile([P, H], U8, name="w1_planes", align_bytes=64)
@@ -162,176 +157,115 @@ def tile_picked_mixup_gelu_p_kernel(
                 out=acc[:, 0 : c1 - c0],
                 lhsT=w1_codes[:, t * P : (t + 1) * P].bitcast(FP8X4),
                 lhsT_scale=w1_planes[:, t * P : (t + 1) * P],
-                rhs=x_codes[c0 // BANK][:, c0 % BANK : c0 % BANK + c1 - c0].bitcast(FP8X4),
-                rhs_scale=x_planes[c0 // BANK][:, c0 % BANK : c0 % BANK + c1 - c0],
+                rhs=x_codes[:, c0:c1].bitcast(FP8X4),
+                rhs_scale=x_planes[:, c0:c1],
                 start=True,
                 stop=True,
             )
             nc.scalar.activation(h[t][:, c0:c1], acc[:, 0 : c1 - c0], ACT.Gelu_apprx_tanh)
 
         for i, (c0, c1) in enumerate(FIRST_PIECES):
-            first_layer(0, c0, c1, (6, 7, 4, 5)[i])
+            first_layer(0, c0, c1, 4 + i)
         for t in range(1, TILES):
             for half in range(2):
-                first_layer(t, half * BANK, (half + 1) * BANK, 4 + (2 * t + half) % 4)
+                first_layer(t, half * BANK, (half + 1) * BANK, 4 + (2 * t + 2 + half) % 4)
 
-        partner = {}
+        partner = [
+            keep.tile([P, TURNED * P], F32, name=f"partner{t}", tag=f"partner{t}", align_bytes=64) for t in range(TILES)
+        ]
 
-        def partner_tile(b0, b1, tag):
-            held = keep.tile([P, TILES, (b1 - b0) * P], F32, name=f"partner{b0}", tag=tag, align_bytes=64)
-            for t in range(TILES):
-                for b in range(b0, b1):
-                    partner[t, b] = (held[:, t, :], (b - b0) * P)
-            return held
+        def gather(t, c0, c1, into, factor):
+            nc.vector.tensor_tensor(into, h[t][:].indirect(pos_sb[:, c0 // 16 : c1 // 16]), factor, ALU.mult)
 
-        def gather(t, c0, c1, factor):
-            row, start = partner[t, c0 // P]
-            nc.vector.tensor_tensor(
-                row[:, start : start + c1 - c0], h[t][:].indirect(pos_sb[:, c0 // 16 : c1 // 16]), factor, ALU.mult
-            )
+        def blocks_of(pair):
+            return range(2 * pair, min(2 * pair + 2, TURNED))
 
-        def gather_turned(t, c0, c1):
-            gather(t, c0, c1, ratio[c0 // BANK][:, c0 % BANK : c0 % BANK + c1 - c0])
+        def sum_bank(pair, u):
+            return pair if u == 0 else 4 + (pair + 2) % 4
 
         sums = {}
 
-        def group(b, t):
-            if b < 4:
-                return (0, 2) if t < 2 else (2, TILES)
-            return 0, TILES
+        def turn(pair, t, source, first, last):
+            u, e = divmod(t, 2)
+            if first:
+                sums[pair, u] = psum.tile([P, 2, 2, P], F32, name="sums", tag=f"bank{sum_bank(pair, u)}")
+            for b in blocks_of(pair):
+                nc.tensor.matmul(
+                    sums[pair, u][:, b % 2, e, :],
+                    source[t][:, b * P : (b + 1) * P],
+                    ident[:],
+                    start=(first and b % 2 == 0),
+                    stop=(last and b == blocks_of(pair)[-1]),
+                    is_transpose=True,
+                )
 
-        def turn_own(b, t):
-            t0, t1 = group(b, t)
-            if t == t0:
-                sums[b, t0] = psum.tile([P, H], F32, name="sums", tag=f"bank{b}")
-            nc.tensor.matmul(
-                sums[b, t0][:, t * P : (t + 1) * P],
-                h[t][:, b * P : (b + 1) * P],
-                ident[:],
-                start=(t == t0),
-                stop=False,
-                is_transpose=True,
-            )
+        z_rows = [keep.tile([P, 2, P, 2], BF16, name=f"z_rows{b}", align_bytes=64) for b in range(TURNED)]
 
-        def turn_partner(b, t):
-            row, start = partner[t, b]
-            t0, t1 = group(b, t)
-            nc.tensor.matmul(
-                sums[b, t0][:, t * P : (t + 1) * P],
-                row[:, start : start + P],
-                ident[:],
-                start=False,
-                stop=(t == t1 - 1),
-                is_transpose=True,
-            )
+        def scale(pair, u):
+            for b in blocks_of(pair):
+                nc.scalar.activation(
+                    z_rows[b][:, u, :, :],
+                    sums[pair, u][:, b % 2, :, :].rearrange("s e p -> s p e"),
+                    ACT.Copy,
+                    scale=own_cols[:, b : b + 1],
+                )
 
-        z_rows = {}
+        z_bf = [keep.tile([P, WIDE, PACK], BF16, name=f"z_bf{pair}", align_bytes=64) for pair in range(PAIRS)]
 
-        def scale(b, t0=0, t1=TILES):
-            if t0 == 0:
-                z_rows[b] = keep.tile([P, 2, P, 2], BF16, name=f"z_rows{b}", tag=f"rows{b}", align_bytes=64)
-            nc.scalar.activation(
-                z_rows[b][:, t0 // 2 : t1 // 2, :, :],
-                sums[b, t0][:, t0 * P : t1 * P].rearrange("s (u e p) -> s u p e", e=2, p=P),
-                ACT.Copy,
-                scale=own_cols[:, b : b + 1],
-            )
+        def turn_back(pair):
+            back = psum.tile([P, 2, 2, P], F32, name="back", tag=f"bank{pair}")
+            count = len(blocks_of(pair))
+            for b in blocks_of(pair):
+                words = z_rows[b][:].rearrange("s u p e -> s (u p e)").bitcast(F32)
+                for u in range(2):
+                    nc.tensor.transpose(back[:, b % 2, u, :], words[:, u * P : (u + 1) * P], ident[:])
+            pairs = z_bf[pair][:].rearrange("p s t -> p (s t)").bitcast(F32).rearrange("p (b s u) -> p b s u", b=2, u=2)
+            nc.scalar.copy(pairs[:, 0:count, :, :], back[:, 0:count, :, :].rearrange("p b u s -> p b s u"))
 
-        z_bf = {c0: keep.tile([P, c1 - c0, PACK], BF16, name=f"z_bf{c0}", align_bytes=64) for c0, c1 in OUT_PIECES}
-
-        def turn_back(b):
-            back = psum.tile([P, PACK, P], F32, name="back", tag=f"bank{b}")
-            words = z_rows[b][:].rearrange("s u p e -> s (u p e)").bitcast(F32)
-            for u in range(2):
-                nc.tensor.transpose(back[:, u, :], words[:, u * P : (u + 1) * P], ident[:])
-            c0 = max(c for c, _ in OUT_PIECES if c <= b * P)
-            pairs = z_bf[c0][:].rearrange("p s t -> p (s t)").bitcast(F32).rearrange("p (s u) -> p s u", u=2)
-            nc.scalar.copy(pairs[:, b * P - c0 : (b + 1) * P - c0, :], back[:, 0:2, :].rearrange("p u s -> p s u"))
-
-        z_mx = {}
-
-        def quantise_z(k, tag):
-            c0, c1 = OUT_PIECES[k]
-            z_codes = keep.tile([P, c1 - c0], U32, name=f"z_codes{c0}", tag=tag, align_bytes=64)
-            z_planes = keep.tile([P, c1 - c0], U8, name=f"z_planes{c0}", align_bytes=64)
+        def second_layer(pair, copy, queue):
+            z_codes = keep.tile([P, WIDE], U32, name=f"z_codes{pair}", align_bytes=64)
+            z_planes = keep.tile([P, WIDE], U8, name=f"z_planes{pair}", align_bytes=64)
             nc.vector.quantize_mx(
-                out=z_codes[:].bitcast(FP8X4), scales=z_planes[:], in_=z_bf[c0][:].rearrange("p c t -> p (c t)")
+                out=z_codes[:].bitcast(FP8X4), scales=z_planes[:], in_=z_bf[pair][:].rearrange("p c t -> p (c t)")
             )
-            z_mx[k] = (z_codes, z_planes)
-
-        def store(k, bank, copy, queue):
-            c0, c1 = OUT_PIECES[k]
-            acc = psum.tile([P, BANK], F32, name="acc", tag=f"bank{bank}")
+            acc = psum.tile([P, BANK], F32, name="acc", tag=f"bank{sum_bank(pair, 1)}")
             nc.tensor.matmul_mx(
-                out=acc[:, 0 : c1 - c0],
+                out=acc[:, 0:WIDE],
                 lhsT=w2_codes[:].bitcast(FP8X4),
                 lhsT_scale=w2_planes[:],
-                rhs=z_mx[k][0][:].bitcast(FP8X4),
-                rhs_scale=z_mx[k][1][:],
+                rhs=z_codes[:].bitcast(FP8X4),
+                rhs_scale=z_planes[:],
                 start=True,
                 stop=True,
             )
-            result = keep.tile([P, c1 - c0], F32, name=f"result{c0}")
-            copy(result[:], acc[:, 0 : c1 - c0])
-            queue.dma_start(out[:, c0:c1], result[:])
+            result = keep.tile([P, WIDE], F32, name=f"result{pair}")
+            copy(result[:], acc[:, 0:WIDE])
+            queue.dma_start(out[:, pair * WIDE : (pair + 1) * WIDE], result[:])
 
-        def mix(b):
-            for t in range(TILES):
-                turn_partner(b, t)
-            scale(b)
-
-        partner_tile(0, 4, "partner0")
-        for t in range(2):
-            gather_turned(t, 0, BANK)
-            for b in range(4):
-                turn_own(b, t)
-            for b in range(4):
-                turn_partner(b, t)
-        gather_turned(2, 0, BANK)
-        for b in range(4):
-            scale(b, 0, 2)
-            turn_own(b, 2)
-            turn_partner(b, 2)
-            turn_own(b, 3)
-        for b0, b1 in ((0, 2), (2, 4)):
-            gather_turned(TILES - 1, b0 * P, b1 * P)
-            for b in range(b0, b1):
-                turn_partner(b, TILES - 1)
-                scale(b, 2, TILES)
-        for b in range(4, TURNED):
-            for t in range(TILES):
-                turn_own(b, t)
-        partner_tile(4, TURNED, "ratio0")
-        for b0, b1 in ((4, 6), (6, 7)):
-            for t in range(TILES):
-                gather_turned(t, b0 * P, b1 * P)
-        turn_back(0)
-        turn_back(1)
-        own_tail = keep.tile([P, TILES, TAIL], F32, name="own_tail", tag="rows1", align_bytes=64)
         for t in range(TILES):
-            nc.vector.tensor_tensor(own_tail[:, t, :], h[t][:, TURNED * P : S], lam_tail[:], ALU.mult)
-        turn_back(2)
-        mix(4)
-        mix(5)
-        turn_back(3)
-        quantise_z(0, "z_codes0")
-        partner_tail = partner_tile(TURNED, BLOCKS, "rows3")
+            for pair in range(PAIRS):
+                turn(pair, t, h, t % 2 == 0, False)
         for t in range(TILES):
-            gather(t, TURNED * P, S, mu_tail[:])
-        mix(6)
-        turn_back(4)
-        turn_back(5)
-        turn_back(6)
-        quantise_z(1, "z_codes1")
+            for c0, c1 in GATHERS[t]:
+                gather(t, c0, c1, partner[t][:, c0:c1], ratio[:, c0:c1])
+            for pair in range(PAIRS):
+                turn(pair, t, partner, False, t % 2 == 1)
+                if t % 2 == 1:
+                    scale(pair, t // 2)
+        tail = keep.tile([P, 2, TILES, TAIL], F32, name="tail", tag="partner2", align_bytes=64)
+        for t in range(TILES):
+            nc.vector.tensor_tensor(tail[:, 0, t, :], h[t][:, TURNED * P : S], lam_tail[:], ALU.mult)
+        for t in range(TILES):
+            gather(t, TURNED * P, S, tail[:, 1, t, :], mu_tail[:])
+        for pair in range(PAIRS):
+            turn_back(pair)
+        second_layer(0, nc.scalar.copy, nc.sync)
         nc.vector.tensor_tensor(
-            z_bf[TURNED * P][:].rearrange("p (c i) t -> p c t i", i=4),
-            own_tail[:].rearrange("p t (c i) -> p c t i", i=4),
-            partner_tail[:].rearrange("p t (c i) -> p c t i", i=4),
+            z_bf[PAIRS - 1][:, WIDE - TAIL : WIDE, :].rearrange("p (c i) t -> p c t i", i=4),
+            tail[:, 0, :, :].rearrange("p t (c i) -> p c t i", i=4),
+            tail[:, 1, :, :].rearrange("p t (c i) -> p c t i", i=4),
             ALU.add,
         )
-        quantise_z(2, "z_codes2")
-        quantise_z(3, "rows6")
-        store(0, 5, nc.scalar.copy, nc.sync)
-        store(1, 0, nc.scalar.copy, nc.sync)
-        store(2, 1, nc.vector.tensor_copy, nc.sync)
-        store(3, 2, nc.scalar.copy, nc.scalar)
+        second_layer(1, nc.scalar.copy, nc.sync)
+        second_layer(2, nc.vector.tensor_copy, nc.sync)
+        second_layer(3, nc.scalar.copy, nc.scalar)

@@ -165,10 +165,10 @@ def tile_picked_mixup_gelu_p_kernel(
             nc.scalar.activation(h[t][:, c0:c1], acc[:, 0 : c1 - c0], ACT.Gelu_apprx_tanh)
 
         for i, (c0, c1) in enumerate(FIRST_PIECES):
-            first_layer(0, c0, c1, 4 + i)
+            first_layer(0, c0, c1, 4 + (i + 1) % 4)
         for t in range(1, TILES):
             for half in range(2):
-                first_layer(t, half * BANK, (half + 1) * BANK, 4 + (2 * t + 2 + half) % 4)
+                first_layer(t, half * BANK, (half + 1) * BANK, 5 + (2 * t - 2 + half) % 3)
 
         partner = [
             keep.tile([P, TURNED * P], F32, name=f"partner{t}", tag=f"partner{t}", align_bytes=64) for t in range(TILES)
@@ -181,7 +181,7 @@ def tile_picked_mixup_gelu_p_kernel(
             return range(2 * pair, min(2 * pair + 2, TURNED))
 
         def sum_bank(pair, u):
-            return pair if u == 0 else 4 + (pair + 2) % 4
+            return pair if u == 0 else 4 + pair
 
         sums = {}
 

@@ -24,10 +24,10 @@ TILES = H // P
 RUN = S // P
 W1_PIECES = ((0, 64), (64, 96), (96, 128))
 FIRST_PIECES = ((0, 256), (256, 512), (512, 768), (768, 1024))
-GATHERS = (((0, 896),), ((0, 512), (512, 896)), ((0, 896),), ((0, 256), (256, 512), (512, 768), (768, 896)))
+GATHERS = (((0, 768),), ((0, 512), (512, 768)), ((0, 768),), ((0, 256), (256, 512), (512, 768)))
 PAIRS = BLOCKS // 2
 WIDE = 2 * P
-TURNED = 7
+TURNED = 6
 TAIL = S - TURNED * P
 
 
@@ -212,7 +212,7 @@ def tile_picked_mixup_gelu_p_kernel(
 
         z_bf = [keep.tile([P, WIDE, PACK], BF16, name=f"z_bf{pair}", align_bytes=64) for pair in range(PAIRS)]
 
-        def turn_back(pair):
+        def turn_back(pair, copy):
             back = psum.tile([P, 2, 2, P], F32, name="back", tag=f"bank{pair}")
             count = len(blocks_of(pair))
             for b in blocks_of(pair):
@@ -220,52 +220,64 @@ def tile_picked_mixup_gelu_p_kernel(
                 for u in range(2):
                     nc.tensor.transpose(back[:, b % 2, u, :], words[:, u * P : (u + 1) * P], ident[:])
             pairs = z_bf[pair][:].rearrange("p s t -> p (s t)").bitcast(F32).rearrange("p (b s u) -> p b s u", b=2, u=2)
-            nc.scalar.copy(pairs[:, 0:count, :, :], back[:, 0:count, :, :].rearrange("p b u s -> p b s u"))
+            copy(pairs[:, 0:count, :, :], back[:, 0:count, :, :].rearrange("p b u s -> p b s u"))
 
-        def second_layer(pair, copy, queue):
+        def second_layer(pair, *ways):
             z_codes = keep.tile([P, WIDE], U32, name=f"z_codes{pair}", align_bytes=64)
             z_planes = keep.tile([P, WIDE], U8, name=f"z_planes{pair}", align_bytes=64)
             nc.vector.quantize_mx(
                 out=z_codes[:].bitcast(FP8X4), scales=z_planes[:], in_=z_bf[pair][:].rearrange("p c t -> p (c t)")
             )
-            acc = psum.tile([P, BANK], F32, name="acc", tag=f"bank{sum_bank(pair, 1)}")
-            nc.tensor.matmul_mx(
-                out=acc[:, 0:WIDE],
-                lhsT=w2_codes[:].bitcast(FP8X4),
-                lhsT_scale=w2_planes[:],
-                rhs=z_codes[:].bitcast(FP8X4),
-                rhs_scale=z_planes[:],
-                start=True,
-                stop=True,
-            )
-            result = keep.tile([P, WIDE], F32, name=f"result{pair}")
-            copy(result[:], acc[:, 0:WIDE])
-            queue.dma_start(out[:, pair * WIDE : (pair + 1) * WIDE], result[:])
+            width = WIDE // len(ways)
+            for i, (bank, copy, queue) in enumerate(ways):
+                c0, c1 = i * width, (i + 1) * width
+                acc = psum.tile([P, BANK], F32, name="acc", tag=f"bank{bank}")
+                nc.tensor.matmul_mx(
+                    out=acc[:, 0:width],
+                    lhsT=w2_codes[:].bitcast(FP8X4),
+                    lhsT_scale=w2_planes[:],
+                    rhs=z_codes[:, c0:c1].bitcast(FP8X4),
+                    rhs_scale=z_planes[:, c0:c1],
+                    start=True,
+                    stop=True,
+                )
+                result = keep.tile([P, width], F32, name=f"result{pair}_{i}")
+                copy(result[:], acc[:, 0:width])
+                queue.dma_start(out[:, pair * WIDE + c0 : pair * WIDE + c1], result[:])
 
+        fetched = keep.tile([P, TILES, TAIL], F32, name="fetched", align_bytes=64)
         for t in range(TILES):
-            for pair in range(PAIRS):
+            nc.scalar.activation(fetched[:, t, :], h[t][:].indirect(pos_sb[:, TURNED * P // 16 : S // 16]), ACT.Copy)
+        for t in range(TILES):
+            for pair in range(TURNED // 2):
                 turn(pair, t, h, t % 2 == 0, False)
         for t in range(TILES):
             for c0, c1 in GATHERS[t]:
                 gather(t, c0, c1, partner[t][:, c0:c1], ratio[:, c0:c1])
-            for pair in range(PAIRS):
+            for pair in range(TURNED // 2):
                 turn(pair, t, partner, False, t % 2 == 1)
                 if t % 2 == 1:
                     scale(pair, t // 2)
         tail = keep.tile([P, 2, TILES, TAIL], F32, name="tail", tag="partner2", align_bytes=64)
         for t in range(TILES):
             nc.vector.tensor_tensor(tail[:, 0, t, :], h[t][:, TURNED * P : S], lam_tail[:], ALU.mult)
-        for t in range(TILES):
-            gather(t, TURNED * P, S, tail[:, 1, t, :], mu_tail[:])
-        for pair in range(PAIRS):
-            turn_back(pair)
-        second_layer(0, nc.scalar.copy, nc.sync)
-        nc.vector.tensor_tensor(
-            z_bf[PAIRS - 1][:, WIDE - TAIL : WIDE, :].rearrange("p (c i) t -> p c t i", i=4),
-            tail[:, 0, :, :].rearrange("p t (c i) -> p c t i", i=4),
-            tail[:, 1, :, :].rearrange("p t (c i) -> p c t i", i=4),
-            ALU.add,
-        )
-        second_layer(1, nc.scalar.copy, nc.sync)
-        second_layer(2, nc.vector.tensor_copy, nc.sync)
-        second_layer(3, nc.scalar.copy, nc.scalar)
+        for c0 in range(0, TAIL, P):
+            nc.vector.tensor_tensor(
+                tail[:, 1, :, c0 : c0 + P],
+                fetched[:, :, c0 : c0 + P],
+                mu_tail[:, c0 : c0 + P].unsqueeze(1).to_broadcast([P, TILES, P]),
+                ALU.mult,
+            )
+        for c0 in range(0, TAIL, P):
+            nc.vector.tensor_tensor(
+                z_bf[PAIRS - 1][:, c0 : c0 + P, :].rearrange("p (c i) t -> p c t i", i=4),
+                tail[:, 0, :, c0 : c0 + P].rearrange("p t (c i) -> p c t i", i=4),
+                tail[:, 1, :, c0 : c0 + P].rearrange("p t (c i) -> p c t i", i=4),
+                ALU.add,
+            )
+        for pair in range(TURNED // 2):
+            turn_back(pair, nc.scalar.copy)
+        second_layer(0, (4, nc.scalar.copy, nc.sync))
+        second_layer(3, (7, nc.scalar.copy, nc.sync))
+        second_layer(1, (5, nc.scalar.copy, nc.sync))
+        second_layer(2, (6, nc.vector.tensor_copy, nc.sync), (3, nc.scalar.copy, nc.scalar))

@@ -249,16 +249,21 @@ def tile_picked_mixup_gelu_p_kernel(
         for t in range(TILES):
             nc.scalar.activation(fetched[:, t, :], h[t][:].indirect(pos_sb[:, TURNED * P // 16 : S // 16]), ACT.Copy)
         for t in range(TILES):
-            for pair in range(TURNED // 2):
-                turn(pair, t, h, t % 2 == 0, False)
-        for t in range(TILES):
             for c0, c1 in GATHERS[t]:
                 gather(t, c0, c1, partner[t][:, c0:c1], ratio[:, c0:c1])
-            for pair in range(TURNED // 2):
-                turn(pair, t, partner, False, t % 2 == 1)
-                if t % 2 == 1:
-                    scale(pair, t // 2)
-        tail = keep.tile([P, 2, TILES, TAIL], F32, name="tail", tag="partner2", align_bytes=64)
+        for pair in range(TURNED // 2):
+            turn(pair, 1, partner, True, False)
+            turn(pair, 0, h, False, False)
+            turn(pair, 1, h, False, False)
+            turn(pair, 0, partner, False, True)
+            scale(pair, 0)
+        for pair in range(TURNED // 2):
+            turn(pair, 2, partner, True, False)
+            turn(pair, 2, h, False, False)
+            turn(pair, 3, h, False, False)
+            turn(pair, 3, partner, False, True)
+            scale(pair, 1)
+        tail = keep.tile([P, 2, TILES, TAIL], F32, name="tail", tag="partner0", align_bytes=64)
         for t in range(TILES):
             nc.vector.tensor_tensor(tail[:, 0, t, :], h[t][:, TURNED * P : S], lam_tail[:], ALU.mult)
         for c0 in range(0, TAIL, P):
@@ -279,5 +284,5 @@ def tile_picked_mixup_gelu_p_kernel(
             turn_back(pair, nc.scalar.copy)
         second_layer(0, (4, nc.scalar.copy, nc.sync))
         second_layer(3, (7, nc.scalar.copy, nc.sync))
-        second_layer(1, (5, nc.scalar.copy, nc.sync))
-        second_layer(2, (6, nc.vector.tensor_copy, nc.sync), (3, nc.scalar.copy, nc.scalar))
+        second_layer(1, (5, nc.vector.tensor_copy, nc.sync))
+        second_layer(2, (6, nc.scalar.copy, nc.scalar))

@@ -19,16 +19,19 @@ ALU = mybir.AluOpType
 P = 128
 PACK = 4
 BANK = 512
-BLOCKS = S // P
+LIST = 16
 TILES = H // P
 RUN = S // P
-W1_PIECES = ((0, 64), (64, 96), (96, 128))
-FIRST_PIECES = ((0, 256), (256, 512), (512, 768), (768, 1024))
-GATHERS = (((0, 768),), ((0, 512), (512, 768)), ((0, 768),), ((0, 256), (256, 512), (512, 768)))
-PAIRS = BLOCKS // 2
 WIDE = 2 * P
+PAIRS = S // WIDE
 TURNED = 6
-TAIL = S - TURNED * P
+TURNED_PAIRS = TURNED // 2
+LAST_PAIR = PAIRS - 1
+TAIL = TURNED * P
+W1_PIECES = ((0, 64), (64, 96), (96, 128))
+FIRST_WIDTH = 256
+GATHERS = (((0, TAIL),), ((0, 2 * WIDE), (2 * WIDE, TAIL)), ((0, TAIL),), ((0, WIDE), (WIDE, 2 * WIDE), (2 * WIDE, TAIL)))
+NUDGES = (2.0**-60, 2.0**-100)
 
 
 def tile_picked_mixup_gelu_p_kernel(
@@ -39,17 +42,17 @@ def tile_picked_mixup_gelu_p_kernel(
         keep = ctx.enter_context(tc.tile_pool(name="keep", bufs=1))
         psum = ctx.enter_context(tc.psum_pool(name="psum", bufs=1))
 
-        offs_sb = keep.tile([P, S // 16], U16, name="offs_sb")
-        pos_sb = keep.tile([P, S // 16], U16, name="pos_sb")
+        offs_sb = keep.tile([P, S // LIST], U16, name="offs_sb")
+        pos_sb = keep.tile([P, S // LIST], U16, name="pos_sb")
         words_all = keep.tile([P, T], U32, name="words_all", align_bytes=64)
         scales_all = keep.tile([P, T], U8, name="scales_all", align_bytes=64)
         w1_raw = [keep.tile([P, PACK, PACK * (m1 - m0)], F32, name=f"w1_raw{m0}", align_bytes=64) for m0, m1 in W1_PIECES]
         w2_raw = keep.tile([P, PACK, N], F32, name="w2_raw")
-        share_rows = keep.tile([P, P], F32, name="share_rows")
+        lam_rows = keep.tile([P, P], F32, name="lam_rows")
         lam_runs = keep.tile([P, RUN], F32, name="lam_runs")
         mu_runs = keep.tile([P, RUN], F32, name="mu_runs")
-        lam_tail = keep.tile([P, TAIL], F32, name="lam_tail")
-        mu_tail = keep.tile([P, TAIL], F32, name="mu_tail")
+        lam_tail = keep.tile([P, WIDE], F32, name="lam_tail")
+        mu_tail = keep.tile([P, WIDE], F32, name="mu_tail")
         ident = keep.tile([P, P], F32, name="ident")
         ones = keep.tile([P, P], F32, name="ones")
         base = keep.tile([P, 1], F32, name="base")
@@ -58,9 +61,10 @@ def tile_picked_mixup_gelu_p_kernel(
         warm = keep.tile([P, 1], F32, name="warm")
 
         nc.gpsimd.memset(scales_all[:].bitcast(I32), 0)
-        nc.gpsimd.memset(share_rows[:], 0.0)
+        nc.gpsimd.memset(lam_rows[:], 0.0)
         nc.vector.memset(ones[:], 1.0)
         nc.scalar.activation(warm[:], ones[:, 0:1], ACT.Gelu_apprx_tanh)
+
         w1_view = w1.rearrange("(p j) c -> p j c", j=PACK)
         nc.sync.dma_start(lam_runs[:], lam[0].rearrange("(p c) -> p c", c=RUN))
         nc.sync.dma_start(mu_runs[:], mu[0].rearrange("(p c) -> p c", c=RUN))
@@ -70,13 +74,14 @@ def tile_picked_mixup_gelu_p_kernel(
                 scales_all[32 * q : 32 * q + 4, :].bitcast(I32), x_scales[0, 4 * q : 4 * q + 4, :].bitcast(I32)
             )
         nc.sync.dma_start(words_all[:].bitcast(I32), x_words[0].rearrange("p n t -> p (n t)").bitcast(I32))
-        nc.sync.dma_start(share_rows[0:BLOCKS, :], lam[0].rearrange("(b p) -> b p", p=P))
+        nc.sync.dma_start(lam_rows[0:TURNED, :], lam[0, 0:TAIL].rearrange("(b p) -> b p", p=P))
         for i, (m0, m1) in enumerate(W1_PIECES):
             nc.sync.dma_start(w1_raw[i][:], w1_view[:, :, PACK * m0 : PACK * m1])
         nc.sync.dma_start(pos_sb[:], pos1)
         nc.sync.dma_start(w2_raw[:], w2.rearrange("(p j) c -> p j c", j=PACK))
-        nc.sync.dma_start(lam_tail[:], lam[:, TURNED * P : S])
-        nc.sync.dma_start(mu_tail[:], mu[:, TURNED * P : S])
+        nc.sync.dma_start(lam_tail[:], lam[:, TAIL:S])
+        nc.sync.dma_start(mu_tail[:], mu[:, TAIL:S])
+
         for q in range(4):
             nc.vector.memset(base[32 * q : 32 * q + 32, :], 32.0 * q)
         nc.vector.tensor_tensor_scan(counts[:], ones[:], ones[:], base[:], ALU.mult, ALU.add)
@@ -86,65 +91,63 @@ def tile_picked_mixup_gelu_p_kernel(
         own_runs = keep.tile([P, RUN], F32, name="own_runs")
         inv_runs = keep.tile([P, RUN], F32, name="inv_runs")
         ratio_runs = keep.tile([P, RUN], F32, name="ratio_runs")
-        nc.vector.tensor_scalar(own_runs[:], lam_runs[:], 2.0**-60, 2.0**-100, ALU.add, ALU.add)
+        nc.vector.tensor_scalar(own_runs[:], lam_runs[:], NUDGES[0], NUDGES[1], ALU.add, ALU.add)
         nc.vector.reciprocal(inv_runs[:], own_runs[:])
         nc.vector.tensor_tensor(ratio_runs[:], mu_runs[:], inv_runs[:], ALU.mult)
-        ratio = keep.tile([P, TURNED * P], F32, name="ratio", align_bytes=64)
-        for quad in range(2):
-            spread = psum.tile([P, PACK, P], F32, name="spread", tag=f"bank{quad}")
-            for i in range(PACK):
-                c = quad * PACK + i
+        ratio = keep.tile([P, TAIL], F32, name="ratio", align_bytes=64)
+        per_bank = BANK // P
+        for bank in range(RUN // per_bank):
+            spread = psum.tile([P, per_bank, P], F32, name="spread", tag=f"bank{bank}")
+            for i in range(per_bank):
+                c = bank * per_bank + i
                 nc.tensor.transpose(spread[:, i, :], ratio_runs[:, c : c + 1].to_broadcast([P, P]), ident[:])
             nc.scalar.copy(
-                ratio[:].rearrange("q (n c) -> q n c", c=RUN)[:, :, quad * PACK : (quad + 1) * PACK],
-                spread[:, :, 0 : TURNED * P // RUN].rearrange("q i n -> q n i"),
+                ratio[:].rearrange("q (n c) -> q n c", c=RUN)[:, :, bank * per_bank : (bank + 1) * per_bank],
+                spread[:, :, 0 : TAIL // RUN].rearrange("q i n -> q n i"),
             )
-        shares = psum.tile([P, BANK], F32, name="shares", tag="bank3")
-        nc.tensor.transpose(shares[:, 0:P], share_rows[:], ident[:])
-        nudged = keep.tile([P, BLOCKS], F32, name="nudged")
-        own_cols = keep.tile([P, BLOCKS], F32, name="own_cols")
-        nc.scalar.activation(nudged[:], shares[:, 0:BLOCKS], ACT.Copy, bias=2.0**-60)
-        nc.scalar.activation(own_cols[:], nudged[:], ACT.Copy, bias=2.0**-100)
+        lam_cols = psum.tile([P, BANK], F32, name="lam_cols", tag="bank3")
+        nc.tensor.transpose(lam_cols[:, 0:P], lam_rows[:], ident[:])
+        nudged = keep.tile([P, TURNED], F32, name="nudged")
+        own_cols = keep.tile([P, TURNED], F32, name="own_cols")
+        nc.scalar.activation(nudged[:], lam_cols[:, 0:TURNED], ACT.Copy, bias=NUDGES[0])
+        nc.scalar.activation(own_cols[:], nudged[:], ACT.Copy, bias=NUDGES[1])
 
-        x_planes = keep.tile([P, S], U8, name="x_planes", align_bytes=64)
+        x_scale = keep.tile([P, S], U8, name="x_scale", align_bytes=64)
         x_codes = keep.tile([P, S], U32, name="x_codes", align_bytes=64)
-        nc.vector.tensor_copy(x_planes[:], scales_all[:].indirect(offs_sb[:]))
+        nc.vector.tensor_copy(x_scale[:], scales_all[:].indirect(offs_sb[:]))
         nc.vector.tensor_copy(x_codes[:], words_all[:].indirect(offs_sb[:]))
 
         w1_codes = keep.tile([P, H], U32, name="w1_codes", align_bytes=64)
-        w1_planes = keep.tile([P, H], U8, name="w1_planes", align_bytes=64)
+        w1_scale = keep.tile([P, H], U8, name="w1_scale", align_bytes=64)
         w1_bf = {}
 
-        def round_w1(u, piece, copy):
-            m0, m1 = W1_PIECES[piece]
-            if piece == 0:
-                w1_bf[u] = keep.tile([P, 2, P, PACK], BF16, name=f"w1_bf{u}", tag="w1_bf", align_bytes=64)
-            copy(
-                w1_bf[u][:, :, m0:m1, :].rearrange("p e m j -> p m j e"),
-                w1_raw[piece][:].rearrange("p j (m t) -> p m j t", t=PACK)[:, :, :, 2 * u : 2 * u + 2],
-            )
+        def round_w1(u, copy):
+            w1_bf[u] = keep.tile([P, 2, P, PACK], BF16, name=f"w1_bf{u}", tag="w1_bf", align_bytes=64)
+            for raw, (m0, m1) in zip(w1_raw, W1_PIECES):
+                copy(
+                    w1_bf[u][:, :, m0:m1, :].rearrange("p e m j -> p m j e"),
+                    raw[:].rearrange("p j (m t) -> p m j t", t=PACK)[:, :, :, 2 * u : 2 * u + 2],
+                )
 
         def quantise_w1(t):
             nc.vector.quantize_mx(
                 out=w1_codes[:, t * P : (t + 1) * P].bitcast(FP8X4),
-                scales=w1_planes[:, t * P : (t + 1) * P],
+                scales=w1_scale[:, t * P : (t + 1) * P],
                 in_=w1_bf[t // 2][:, t % 2, :, :].rearrange("p m j -> p (m j)"),
             )
 
-        for piece in range(len(W1_PIECES)):
-            round_w1(0, piece, nc.scalar.copy)
+        round_w1(0, nc.scalar.copy)
         quantise_w1(0)
         quantise_w1(1)
         w2_bf = keep.tile([P, N, PACK], BF16, name="w2_bf", align_bytes=64)
         nc.vector.tensor_copy(
             w2_bf[:].rearrange("p (c i) j -> p c j i", i=4), w2_raw[:].rearrange("p j (c i) -> p c j i", i=4)
         )
-        for piece in range(len(W1_PIECES)):
-            round_w1(1, piece, nc.vector.tensor_copy)
+        round_w1(1, nc.vector.tensor_copy)
         w2_codes = keep.tile([P, N], U32, name="w2_codes", align_bytes=64)
-        w2_planes = keep.tile([P, N], U8, name="w2_planes", align_bytes=64)
+        w2_scale = keep.tile([P, N], U8, name="w2_scale", align_bytes=64)
         nc.vector.quantize_mx(
-            out=w2_codes[:].bitcast(FP8X4), scales=w2_planes[:], in_=w2_bf[:].rearrange("p n j -> p (n j)")
+            out=w2_codes[:].bitcast(FP8X4), scales=w2_scale[:], in_=w2_bf[:].rearrange("p n j -> p (n j)")
         )
         quantise_w1(2)
         quantise_w1(3)
@@ -156,133 +159,107 @@ def tile_picked_mixup_gelu_p_kernel(
             nc.tensor.matmul_mx(
                 out=acc[:, 0 : c1 - c0],
                 lhsT=w1_codes[:, t * P : (t + 1) * P].bitcast(FP8X4),
-                lhsT_scale=w1_planes[:, t * P : (t + 1) * P],
+                lhsT_scale=w1_scale[:, t * P : (t + 1) * P],
                 rhs=x_codes[:, c0:c1].bitcast(FP8X4),
-                rhs_scale=x_planes[:, c0:c1],
+                rhs_scale=x_scale[:, c0:c1],
                 start=True,
                 stop=True,
             )
             nc.scalar.activation(h[t][:, c0:c1], acc[:, 0 : c1 - c0], ACT.Gelu_apprx_tanh)
 
-        for i, (c0, c1) in enumerate(FIRST_PIECES):
-            first_layer(0, c0, c1, 4 + (i + 1) % 4)
-        for t in range(1, TILES):
-            for half in range(2):
-                first_layer(t, half * BANK, (half + 1) * BANK, 5 + (2 * t - 2 + half) % 3)
+        for i, bank in enumerate((5, 6, 7, 4)):
+            first_layer(0, i * FIRST_WIDTH, (i + 1) * FIRST_WIDTH, bank)
+        for i in range(2 * (TILES - 1)):
+            first_layer(1 + i // 2, i % 2 * BANK, (i % 2 + 1) * BANK, 5 + i % 3)
 
-        partner = [
-            keep.tile([P, TURNED * P], F32, name=f"partner{t}", tag=f"partner{t}", align_bytes=64) for t in range(TILES)
-        ]
+        partner = [keep.tile([P, TAIL], F32, name=f"partner{t}", tag=f"partner{t}", align_bytes=64) for t in range(TILES)]
+        z_rows = [keep.tile([P, 2, P, 2], BF16, name=f"z_rows{b}", tag=f"z_rows{b}", align_bytes=64) for b in range(TURNED)]
+        z_bf = [keep.tile([P, WIDE, PACK], BF16, name=f"z_bf{pair}", align_bytes=64) for pair in range(PAIRS)]
+        fetched = keep.tile([P, TILES, WIDE], F32, name="fetched", align_bytes=64)
+        for t in range(TILES):
+            nc.scalar.activation(fetched[:, t, :], h[t][:].indirect(pos_sb[:, TAIL // LIST : S // LIST]), ACT.Copy)
 
-        def gather(t, c0, c1, into, factor):
-            nc.vector.tensor_tensor(into, h[t][:].indirect(pos_sb[:, c0 // 16 : c1 // 16]), factor, ALU.mult)
-
-        def blocks_of(pair):
-            return range(2 * pair, min(2 * pair + 2, TURNED))
-
-        def sum_bank(pair, u):
-            return pair if u == 0 else 4 + pair
-
-        sums = {}
-
-        def turn(pair, t, source, first, last):
-            u, e = divmod(t, 2)
-            if first:
-                sums[pair, u] = psum.tile([P, 2, 2, P], F32, name="sums", tag=f"bank{sum_bank(pair, u)}")
-            for b in blocks_of(pair):
-                nc.tensor.matmul(
-                    sums[pair, u][:, b % 2, e, :],
-                    source[t][:, b * P : (b + 1) * P],
-                    ident[:],
-                    start=(first and b % 2 == 0),
-                    stop=(last and b == blocks_of(pair)[-1]),
-                    is_transpose=True,
+        for t in range(TILES):
+            for c0, c1 in GATHERS[t]:
+                nc.vector.tensor_tensor(
+                    partner[t][:, c0:c1], h[t][:].indirect(pos_sb[:, c0 // LIST : c1 // LIST]), ratio[:, c0:c1], ALU.mult
                 )
 
-        z_rows = [keep.tile([P, 2, P, 2], BF16, name=f"z_rows{b}", align_bytes=64) for b in range(TURNED)]
-
-        def scale(pair, u):
-            for b in blocks_of(pair):
+        def mix_turned(pair, u, terms):
+            sums = psum.tile([P, 2, 2, P], F32, name="sums", tag=f"bank{4 * u + pair}")
+            for i, (source, t) in enumerate(terms):
+                for half in range(2):
+                    b = 2 * pair + half
+                    nc.tensor.matmul(
+                        sums[:, half, t % 2, :],
+                        source[t][:, b * P : (b + 1) * P],
+                        ident[:],
+                        start=(i == 0 and half == 0),
+                        stop=(i == len(terms) - 1 and half == 1),
+                        is_transpose=True,
+                    )
+            for half in range(2):
+                b = 2 * pair + half
                 nc.scalar.activation(
                     z_rows[b][:, u, :, :],
-                    sums[pair, u][:, b % 2, :, :].rearrange("s e p -> s p e"),
+                    sums[:, half, :, :].rearrange("s e p -> s p e"),
                     ACT.Copy,
                     scale=own_cols[:, b : b + 1],
                 )
 
-        z_bf = [keep.tile([P, WIDE, PACK], BF16, name=f"z_bf{pair}", align_bytes=64) for pair in range(PAIRS)]
+        for pair in range(TURNED_PAIRS):
+            mix_turned(pair, 0, ((partner, 1), (h, 0), (h, 1), (partner, 0)))
+        for pair in range(TURNED_PAIRS):
+            mix_turned(pair, 1, ((partner, 2), (h, 2), (h, 3), (partner, 3)))
 
-        def turn_back(pair, copy):
-            back = psum.tile([P, 2, 2, P], F32, name="back", tag=f"bank{pair}")
-            count = len(blocks_of(pair))
-            for b in blocks_of(pair):
-                words = z_rows[b][:].rearrange("s u p e -> s (u p e)").bitcast(F32)
-                for u in range(2):
-                    nc.tensor.transpose(back[:, b % 2, u, :], words[:, u * P : (u + 1) * P], ident[:])
-            pairs = z_bf[pair][:].rearrange("p s t -> p (s t)").bitcast(F32).rearrange("p (b s u) -> p b s u", b=2, u=2)
-            copy(pairs[:, 0:count, :, :], back[:, 0:count, :, :].rearrange("p b u s -> p b s u"))
-
-        def second_layer(pair, *ways):
-            z_codes = keep.tile([P, WIDE], U32, name=f"z_codes{pair}", align_bytes=64)
-            z_planes = keep.tile([P, WIDE], U8, name=f"z_planes{pair}", align_bytes=64)
-            nc.vector.quantize_mx(
-                out=z_codes[:].bitcast(FP8X4), scales=z_planes[:], in_=z_bf[pair][:].rearrange("p c t -> p (c t)")
-            )
-            width = WIDE // len(ways)
-            for i, (bank, copy, queue) in enumerate(ways):
-                c0, c1 = i * width, (i + 1) * width
-                acc = psum.tile([P, BANK], F32, name="acc", tag=f"bank{bank}")
-                nc.tensor.matmul_mx(
-                    out=acc[:, 0:width],
-                    lhsT=w2_codes[:].bitcast(FP8X4),
-                    lhsT_scale=w2_planes[:],
-                    rhs=z_codes[:, c0:c1].bitcast(FP8X4),
-                    rhs_scale=z_planes[:, c0:c1],
-                    start=True,
-                    stop=True,
-                )
-                result = keep.tile([P, width], F32, name=f"result{pair}_{i}")
-                copy(result[:], acc[:, 0:width])
-                queue.dma_start(out[:, pair * WIDE + c0 : pair * WIDE + c1], result[:])
-
-        fetched = keep.tile([P, TILES, TAIL], F32, name="fetched", align_bytes=64)
+        terms = keep.tile([P, 2, TILES, WIDE], F32, name="terms", tag="partner0", align_bytes=64)
         for t in range(TILES):
-            nc.scalar.activation(fetched[:, t, :], h[t][:].indirect(pos_sb[:, TURNED * P // 16 : S // 16]), ACT.Copy)
-        for t in range(TILES):
-            for c0, c1 in GATHERS[t]:
-                gather(t, c0, c1, partner[t][:, c0:c1], ratio[:, c0:c1])
-        for pair in range(TURNED // 2):
-            turn(pair, 1, partner, True, False)
-            turn(pair, 0, h, False, False)
-            turn(pair, 1, h, False, False)
-            turn(pair, 0, partner, False, True)
-            scale(pair, 0)
-        for pair in range(TURNED // 2):
-            turn(pair, 2, partner, True, False)
-            turn(pair, 2, h, False, False)
-            turn(pair, 3, h, False, False)
-            turn(pair, 3, partner, False, True)
-            scale(pair, 1)
-        tail = keep.tile([P, 2, TILES, TAIL], F32, name="tail", tag="partner0", align_bytes=64)
-        for t in range(TILES):
-            nc.vector.tensor_tensor(tail[:, 0, t, :], h[t][:, TURNED * P : S], lam_tail[:], ALU.mult)
-        for c0 in range(0, TAIL, P):
+            nc.vector.tensor_tensor(terms[:, 0, t, :], h[t][:, TAIL:S], lam_tail[:], ALU.mult)
+        for c0 in range(0, WIDE, P):
             nc.vector.tensor_tensor(
-                tail[:, 1, :, c0 : c0 + P],
+                terms[:, 1, :, c0 : c0 + P],
                 fetched[:, :, c0 : c0 + P],
                 mu_tail[:, c0 : c0 + P].unsqueeze(1).to_broadcast([P, TILES, P]),
                 ALU.mult,
             )
-        for c0 in range(0, TAIL, P):
+        for c0 in range(0, WIDE, P):
             nc.vector.tensor_tensor(
-                z_bf[PAIRS - 1][:, c0 : c0 + P, :].rearrange("p (c i) t -> p c t i", i=4),
-                tail[:, 0, :, c0 : c0 + P].rearrange("p t (c i) -> p c t i", i=4),
-                tail[:, 1, :, c0 : c0 + P].rearrange("p t (c i) -> p c t i", i=4),
+                z_bf[LAST_PAIR][:, c0 : c0 + P, :].rearrange("p (c i) t -> p c t i", i=4),
+                terms[:, 0, :, c0 : c0 + P].rearrange("p t (c i) -> p c t i", i=4),
+                terms[:, 1, :, c0 : c0 + P].rearrange("p t (c i) -> p c t i", i=4),
                 ALU.add,
             )
-        for pair in range(TURNED // 2):
-            turn_back(pair, nc.scalar.copy)
-        second_layer(0, (4, nc.scalar.copy, nc.sync))
-        second_layer(3, (7, nc.scalar.copy, nc.sync))
-        second_layer(1, (5, nc.vector.tensor_copy, nc.sync))
-        second_layer(2, (6, nc.scalar.copy, nc.scalar))
+
+        for pair in range(TURNED_PAIRS):
+            back = psum.tile([P, 2, 2, P], F32, name="back", tag=f"bank{pair}")
+            for half in range(2):
+                words = z_rows[2 * pair + half][:].rearrange("s u p e -> s (u p e)").bitcast(F32)
+                for u in range(2):
+                    nc.tensor.transpose(back[:, half, u, :], words[:, u * P : (u + 1) * P], ident[:])
+            z_words = z_bf[pair][:].rearrange("p s t -> p (s t)").bitcast(F32).rearrange("p (b s u) -> p b s u", b=2, u=2)
+            nc.scalar.copy(z_words, back[:].rearrange("p b u s -> p b s u"))
+
+        def second_layer(pair, codes_tag, copy, queue):
+            z_codes = keep.tile([P, WIDE], U32, name=f"z_codes{pair}", tag=codes_tag, align_bytes=64)
+            z_scale = keep.tile([P, WIDE], U8, name=f"z_scale{pair}", align_bytes=64)
+            nc.vector.quantize_mx(
+                out=z_codes[:].bitcast(FP8X4), scales=z_scale[:], in_=z_bf[pair][:].rearrange("p c t -> p (c t)")
+            )
+            acc = psum.tile([P, BANK], F32, name="acc", tag=f"bank{4 + pair}")
+            nc.tensor.matmul_mx(
+                out=acc[:, 0:WIDE],
+                lhsT=w2_codes[:].bitcast(FP8X4),
+                lhsT_scale=w2_scale[:],
+                rhs=z_codes[:].bitcast(FP8X4),
+                rhs_scale=z_scale[:],
+                start=True,
+                stop=True,
+            )
+            result = keep.tile([P, WIDE], F32, name=f"result{pair}")
+            copy(result[:], acc[:, 0:WIDE])
+            queue.dma_start(out[:, pair * WIDE : (pair + 1) * WIDE], result[:])
+
+        second_layer(0, "z_codes0", nc.scalar.copy, nc.sync)
+        second_layer(LAST_PAIR, f"z_rows{TURNED - 1}", nc.scalar.copy, nc.sync)
+        second_layer(1, "z_codes1", nc.vector.tensor_copy, nc.sync)
+        second_layer(2, "z_codes2", nc.scalar.copy, nc.scalar)

@@ -262,4 +262,4 @@ def tile_picked_mixup_gelu_p_kernel(
         second_layer(0, "z_codes0", nc.scalar.copy, nc.sync)
         second_layer(LAST_PAIR, f"z_rows{TURNED - 1}", nc.scalar.copy, nc.sync)
         second_layer(1, "z_codes1", nc.vector.tensor_copy, nc.sync)
-        second_layer(2, "z_codes2", nc.scalar.copy, nc.scalar)
+        second_layer(2, "z_codes2", nc.scalar.copy, nc.sync)

@@ -31,6 +31,7 @@ TAIL = TURNED * P
 W1_PIECES = ((0, 64), (64, 96), (96, 128))
 FIRST_WIDTH = 256
 GATHERS = (((0, TAIL),), ((0, 2 * WIDE), (2 * WIDE, TAIL)), ((0, TAIL),), ((0, WIDE), (WIDE, 2 * WIDE), (2 * WIDE, TAIL)))
+CLEAR = 1280
 NUDGES = (2.0**-60, 2.0**-100)
 
 
@@ -60,9 +61,10 @@ def tile_picked_mixup_gelu_p_kernel(
         row_number = keep.tile([P, 32], F32, name="row_number", align_bytes=64)
         warm = keep.tile([P, 1], F32, name="warm")
 
-        nc.gpsimd.memset(scales_all[:].bitcast(I32), 0)
-        nc.gpsimd.memset(lam_rows[:], 0.0)
         nc.vector.memset(ones[:], 1.0)
+        nc.vector.memset(scales_all[:, 0:CLEAR].bitcast(I32), 0)
+        nc.gpsimd.memset(scales_all[:, CLEAR:T].bitcast(I32), 0)
+        nc.gpsimd.memset(lam_rows[:], 0.0)
         nc.scalar.activation(warm[:], ones[:, 0:1], ACT.Gelu_apprx_tanh)
 
         w1_view = w1.rearrange("(p j) c -> p j c", j=PACK)

@@ -61,10 +61,10 @@ def tile_picked_mixup_gelu_p_kernel(
         row_number = keep.tile([P, 32], F32, name="row_number", align_bytes=64)
         warm = keep.tile([P, 1], F32, name="warm")
 
-        nc.vector.memset(ones[:], 1.0)
         nc.vector.memset(scales_all[:, 0:CLEAR].bitcast(I32), 0)
         nc.gpsimd.memset(scales_all[:, CLEAR:T].bitcast(I32), 0)
         nc.gpsimd.memset(lam_rows[:], 0.0)
+        nc.vector.memset(ones[:], 1.0)
         nc.scalar.activation(warm[:], ones[:, 0:1], ACT.Gelu_apprx_tanh)
 
         w1_view = w1.rearrange("(p j) c -> p j c", j=PACK)

@@ -28,10 +28,10 @@ TURNED = 6
 TURNED_PAIRS = TURNED // 2
 LAST_PAIR = PAIRS - 1
 TAIL = TURNED * P
-W1_PIECES = ((0, 64), (64, 96), (96, 128))
+W1_PIECES = ((0, 48), (48, 96), (96, 128))
+WORD_CUT = 768
 FIRST_WIDTH = 256
 GATHERS = (((0, TAIL),), ((0, 2 * WIDE), (2 * WIDE, TAIL)), ((0, TAIL),), ((0, WIDE), (WIDE, 2 * WIDE), (2 * WIDE, TAIL)))
-CLEAR = 1280
 NUDGES = (2.0**-60, 2.0**-100)
 
 
@@ -41,15 +41,17 @@ def tile_picked_mixup_gelu_p_kernel(
     nc = tc.nc
     with ExitStack() as ctx:
         keep = ctx.enter_context(tc.tile_pool(name="keep", bufs=1))
+        late = ctx.enter_context(tc.tile_pool(name="late", bufs=1))
         psum = ctx.enter_context(tc.psum_pool(name="psum", bufs=1))
 
         offs_sb = keep.tile([P, S // LIST], U16, name="offs_sb")
         pos_sb = keep.tile([P, S // LIST], U16, name="pos_sb")
         words_all = keep.tile([P, T], U32, name="words_all", align_bytes=64)
         scales_all = keep.tile([P, T], U8, name="scales_all", align_bytes=64)
-        w1_raw = [keep.tile([P, PACK, PACK * (m1 - m0)], F32, name=f"w1_raw{m0}", align_bytes=64) for m0, m1 in W1_PIECES]
+        w1_raw = [keep.tile([P, PACK, PACK * (m1 - m0)], F32, name=f"w1_raw{m0}", align_bytes=64) for m0, m1 in W1_PIECES[:2]]
+        w1_raw.append(late.tile([P, PACK, PACK * (W1_PIECES[2][1] - W1_PIECES[2][0])], F32, name="w1_last", offset=0, align_bytes=64))
         w2_raw = keep.tile([P, PACK, N], F32, name="w2_raw")
-        lam_rows = keep.tile([P, P], F32, name="lam_rows")
+        lam_cols = keep.tile([P, TURNED], F32, name="lam_cols")
         lam_runs = keep.tile([P, RUN], F32, name="lam_runs")
         mu_runs = keep.tile([P, RUN], F32, name="mu_runs")
         lam_tail = keep.tile([P, WIDE], F32, name="lam_tail")
@@ -61,26 +63,31 @@ def tile_picked_mixup_gelu_p_kernel(
         row_number = keep.tile([P, 32], F32, name="row_number", align_bytes=64)
         warm = keep.tile([P, 1], F32, name="warm")
 
-        nc.vector.memset(scales_all[:, 0:CLEAR].bitcast(I32), 0)
-        nc.gpsimd.memset(scales_all[:, CLEAR:T].bitcast(I32), 0)
-        nc.gpsimd.memset(lam_rows[:], 0.0)
+        nc.vector.memset(scales_all[:].bitcast(I32), 0)
         nc.vector.memset(ones[:], 1.0)
         nc.scalar.activation(warm[:], ones[:, 0:1], ACT.Gelu_apprx_tanh)
 
         w1_view = w1.rearrange("(p j) c -> p j c", j=PACK)
+
+        def load_w1(i):
+            m0, m1 = W1_PIECES[i]
+            nc.sync.dma_start(w1_raw[i][:], w1_view[:, :, PACK * m0 : PACK * m1])
+
+        load_w1(0)
         nc.sync.dma_start(lam_runs[:], lam[0].rearrange("(p c) -> p c", c=RUN))
-        nc.sync.dma_start(mu_runs[:], mu[0].rearrange("(p c) -> p c", c=RUN))
         nc.sync.dma_start(offs_sb[:], offs)
         for q in range(4):
             nc.sync.dma_start(
                 scales_all[32 * q : 32 * q + 4, :].bitcast(I32), x_scales[0, 4 * q : 4 * q + 4, :].bitcast(I32)
             )
         nc.sync.dma_start(words_all[:].bitcast(I32), x_words[0].rearrange("p n t -> p (n t)").bitcast(I32))
-        nc.sync.dma_start(lam_rows[0:TURNED, :], lam[0, 0:TAIL].rearrange("(b p) -> b p", p=P))
-        for i, (m0, m1) in enumerate(W1_PIECES):
-            nc.sync.dma_start(w1_raw[i][:], w1_view[:, :, PACK * m0 : PACK * m1])
+        nc.sync.dma_start(mu_runs[:], mu[0].rearrange("(p c) -> p c", c=RUN))
+        load_w1(1)
+        load_w1(2)
         nc.sync.dma_start(pos_sb[:], pos1)
         nc.sync.dma_start(w2_raw[:], w2.rearrange("(p j) c -> p j c", j=PACK))
+        with nc.allow_non_contiguous_dma(reason="one value a partition and block"):
+            nc.sync.dma_start(lam_cols[:], lam[0, 0:TAIL].rearrange("(b s) -> s b", s=P))
         nc.sync.dma_start(lam_tail[:], lam[:, TAIL:S])
         nc.sync.dma_start(mu_tail[:], mu[:, TAIL:S])
 
@@ -95,8 +102,28 @@ def tile_picked_mixup_gelu_p_kernel(
         ratio_runs = keep.tile([P, RUN], F32, name="ratio_runs")
         nc.vector.tensor_scalar(own_runs[:], lam_runs[:], NUDGES[0], NUDGES[1], ALU.add, ALU.add)
         nc.vector.reciprocal(inv_runs[:], own_runs[:])
-        nc.vector.tensor_tensor(ratio_runs[:], mu_runs[:], inv_runs[:], ALU.mult)
-        ratio = keep.tile([P, TAIL], F32, name="ratio", align_bytes=64)
+
+        w1_bf = keep.tile([P, TILES, P, PACK], BF16, name="w1_bf", align_bytes=64)
+
+        def round_w1(i, t0, t1, copy):
+            m0, m1 = W1_PIECES[i]
+            copy(
+                w1_bf[:, t0:t1, m0:m1, :].rearrange("p t m j -> p m j t"),
+                w1_raw[i][:].rearrange("p j (m t) -> p m j t", t=PACK)[:, :, :, t0:t1],
+            )
+
+        round_w1(0, 0, TILES, nc.scalar.copy)
+        for c in range(RUN):
+            nc.scalar.activation(ratio_runs[:, c : c + 1], mu_runs[:, c : c + 1], ACT.Copy, scale=inv_runs[:, c : c + 1])
+        round_w1(1, 0, 2, nc.scalar.copy)
+        round_w1(2, 0, TILES, nc.scalar.copy)
+
+        x_scale = keep.tile([P, S], U8, name="x_scale", align_bytes=64)
+        x_head = keep.tile([P, WORD_CUT], U32, name="x_head", align_bytes=64)
+        nc.vector.tensor_copy(x_scale[:], scales_all[:].indirect(offs_sb[:]))
+        nc.vector.tensor_copy(x_head[:], words_all[:].indirect(offs_sb[:, 0 : WORD_CUT // LIST]))
+
+        ratio = late.tile([P, TAIL], F32, name="ratio", offset=4 * (S - WORD_CUT), align_bytes=64)
         per_bank = BANK // P
         for bank in range(RUN // per_bank):
             spread = psum.tile([P, per_bank, P], F32, name="spread", tag=f"bank{bank}")
@@ -107,66 +134,52 @@ def tile_picked_mixup_gelu_p_kernel(
                 ratio[:].rearrange("q (n c) -> q n c", c=RUN)[:, :, bank * per_bank : (bank + 1) * per_bank],
                 spread[:, :, 0 : TAIL // RUN].rearrange("q i n -> q n i"),
             )
-        lam_cols = psum.tile([P, BANK], F32, name="lam_cols", tag="bank3")
-        nc.tensor.transpose(lam_cols[:, 0:P], lam_rows[:], ident[:])
-        nudged = keep.tile([P, TURNED], F32, name="nudged")
-        own_cols = keep.tile([P, TURNED], F32, name="own_cols")
-        nc.scalar.activation(nudged[:], lam_cols[:, 0:TURNED], ACT.Copy, bias=NUDGES[0])
-        nc.scalar.activation(own_cols[:], nudged[:], ACT.Copy, bias=NUDGES[1])
-
-        x_scale = keep.tile([P, S], U8, name="x_scale", align_bytes=64)
-        x_codes = keep.tile([P, S], U32, name="x_codes", align_bytes=64)
-        nc.vector.tensor_copy(x_scale[:], scales_all[:].indirect(offs_sb[:]))
-        nc.vector.tensor_copy(x_codes[:], words_all[:].indirect(offs_sb[:]))
 
         w1_codes = keep.tile([P, H], U32, name="w1_codes", align_bytes=64)
         w1_scale = keep.tile([P, H], U8, name="w1_scale", align_bytes=64)
-        w1_bf = {}
-
-        def round_w1(u, copy):
-            w1_bf[u] = keep.tile([P, 2, P, PACK], BF16, name=f"w1_bf{u}", tag="w1_bf", align_bytes=64)
-            for raw, (m0, m1) in zip(w1_raw, W1_PIECES):
-                copy(
-                    w1_bf[u][:, :, m0:m1, :].rearrange("p e m j -> p m j e"),
-                    raw[:].rearrange("p j (m t) -> p m j t", t=PACK)[:, :, :, 2 * u : 2 * u + 2],
-                )
 
         def quantise_w1(t):
             nc.vector.quantize_mx(
                 out=w1_codes[:, t * P : (t + 1) * P].bitcast(FP8X4),
                 scales=w1_scale[:, t * P : (t + 1) * P],
-                in_=w1_bf[t // 2][:, t % 2, :, :].rearrange("p m j -> p (m j)"),
+                in_=w1_bf[:, t, :, :].rearrange("p m j -> p (m j)"),
             )
 
-        round_w1(0, nc.scalar.copy)
         quantise_w1(0)
+        x_rest = late.tile([P, S - WORD_CUT], U32, name="x_rest", offset=0, align_bytes=64)
+        nc.vector.tensor_copy(x_rest[:], words_all[:].indirect(offs_sb[:, WORD_CUT // LIST : S // LIST]))
         quantise_w1(1)
+        round_w1(1, 2, TILES, nc.vector.tensor_copy)
         w2_bf = keep.tile([P, N, PACK], BF16, name="w2_bf", align_bytes=64)
         nc.vector.tensor_copy(
             w2_bf[:].rearrange("p (c i) j -> p c j i", i=4), w2_raw[:].rearrange("p j (c i) -> p c j i", i=4)
         )
-        round_w1(1, nc.vector.tensor_copy)
+        own_cols = keep.tile([P, TURNED], F32, name="own_cols")
+        nc.vector.tensor_scalar(own_cols[:], lam_cols[:], NUDGES[0], NUDGES[1], ALU.add, ALU.add)
+        quantise_w1(2)
+        quantise_w1(3)
         w2_codes = keep.tile([P, N], U32, name="w2_codes", align_bytes=64)
         w2_scale = keep.tile([P, N], U8, name="w2_scale", align_bytes=64)
         nc.vector.quantize_mx(
             out=w2_codes[:].bitcast(FP8X4), scales=w2_scale[:], in_=w2_bf[:].rearrange("p n j -> p (n j)")
         )
-        quantise_w1(2)
-        quantise_w1(3)
 
         h = [keep.tile([P, S], F32, name=f"h{t}", align_bytes=64) for t in range(TILES)]
 
         def first_layer(t, c0, c1, bank):
             acc = psum.tile([P, BANK], F32, name="acc", tag=f"bank{bank}")
-            nc.tensor.matmul_mx(
-                out=acc[:, 0 : c1 - c0],
-                lhsT=w1_codes[:, t * P : (t + 1) * P].bitcast(FP8X4),
-                lhsT_scale=w1_scale[:, t * P : (t + 1) * P],
-                rhs=x_codes[:, c0:c1].bitcast(FP8X4),
-                rhs_scale=x_scale[:, c0:c1],
-                start=True,
-                stop=True,
-            )
+            cuts = (c0, WORD_CUT, c1) if c0 < WORD_CUT < c1 else (c0, c1)
+            for a, b in zip(cuts, cuts[1:]):
+                codes = x_head[:, a:b] if b <= WORD_CUT else x_rest[:, a - WORD_CUT : b - WORD_CUT]
+                nc.tensor.matmul_mx(
+                    out=acc[:, a - c0 : b - c0],
+                    lhsT=w1_codes[:, t * P : (t + 1) * P].bitcast(FP8X4),
+                    lhsT_scale=w1_scale[:, t * P : (t + 1) * P],
+                    rhs=codes.bitcast(FP8X4),
+                    rhs_scale=x_scale[:, a:b],
+                    start=True,
+                    stop=True,
+                )
             nc.scalar.activation(h[t][:, c0:c1], acc[:, 0 : c1 - c0], ACT.Gelu_apprx_tanh)
 
         for i, bank in enumerate((5, 6, 7, 4)):

@@ -103,7 +103,7 @@ def tile_picked_mixup_gelu_p_kernel(
         nc.vector.tensor_scalar(own_runs[:], lam_runs[:], NUDGES[0], NUDGES[1], ALU.add, ALU.add)
         nc.vector.reciprocal(inv_runs[:], own_runs[:])
 
-        w1_bf = keep.tile([P, TILES, P, PACK], BF16, name="w1_bf", align_bytes=64)
+        w1_bf = keep.tile([P, TILES + 1, P, PACK], BF16, name="w1_bf", align_bytes=64)
 
         def round_w1(i, t0, t1, copy):
             m0, m1 = W1_PIECES[i]
@@ -135,34 +135,27 @@ def tile_picked_mixup_gelu_p_kernel(
                 spread[:, :, 0 : TAIL // RUN].rearrange("q i n -> q n i"),
             )
 
-        w1_codes = keep.tile([P, H], U32, name="w1_codes", align_bytes=64)
-        w1_scale = keep.tile([P, H], U8, name="w1_scale", align_bytes=64)
+        w1_codes = keep.tile([P, H + N], U32, name="w1_codes", align_bytes=64)
+        w1_scale = keep.tile([P, H + N], U8, name="w1_scale", align_bytes=64)
 
-        def quantise_w1(t):
+        def quantise_w1(t0, t1):
             nc.vector.quantize_mx(
-                out=w1_codes[:, t * P : (t + 1) * P].bitcast(FP8X4),
-                scales=w1_scale[:, t * P : (t + 1) * P],
-                in_=w1_bf[:, t, :, :].rearrange("p m j -> p (m j)"),
+                out=w1_codes[:, t0 * P : t1 * P].bitcast(FP8X4),
+                scales=w1_scale[:, t0 * P : t1 * P],
+                in_=w1_bf[:, t0:t1, :, :].rearrange("p t m j -> p (t m j)"),
             )
 
-        quantise_w1(0)
+        quantise_w1(0, 1)
         x_rest = late.tile([P, S - WORD_CUT], U32, name="x_rest", offset=0, align_bytes=64)
         nc.vector.tensor_copy(x_rest[:], words_all[:].indirect(offs_sb[:, WORD_CUT // LIST : S // LIST]))
-        quantise_w1(1)
+        quantise_w1(1, 2)
         round_w1(1, 2, TILES, nc.vector.tensor_copy)
-        w2_bf = keep.tile([P, N, PACK], BF16, name="w2_bf", align_bytes=64)
         nc.vector.tensor_copy(
-            w2_bf[:].rearrange("p (c i) j -> p c j i", i=4), w2_raw[:].rearrange("p j (c i) -> p c j i", i=4)
+            w1_bf[:, TILES, :, :].rearrange("p (c i) j -> p c j i", i=4), w2_raw[:].rearrange("p j (c i) -> p c j i", i=4)
         )
         own_cols = keep.tile([P, TURNED], F32, name="own_cols")
         nc.vector.tensor_scalar(own_cols[:], lam_cols[:], NUDGES[0], NUDGES[1], ALU.add, ALU.add)
-        quantise_w1(2)
-        quantise_w1(3)
-        w2_codes = keep.tile([P, N], U32, name="w2_codes", align_bytes=64)
-        w2_scale = keep.tile([P, N], U8, name="w2_scale", align_bytes=64)
-        nc.vector.quantize_mx(
-            out=w2_codes[:].bitcast(FP8X4), scales=w2_scale[:], in_=w2_bf[:].rearrange("p n j -> p (n j)")
-        )
+        quantise_w1(2, TILES + 1)
 
         h = [keep.tile([P, S], F32, name=f"h{t}", align_bytes=64) for t in range(TILES)]
 
@@ -189,7 +182,7 @@ def tile_picked_mixup_gelu_p_kernel(
 
         partner = [keep.tile([P, TAIL], F32, name=f"partner{t}", tag=f"partner{t}", align_bytes=64) for t in range(TILES)]
         z_rows = [keep.tile([P, 2, P, 2], BF16, name=f"z_rows{b}", tag=f"z_rows{b}", align_bytes=64) for b in range(TURNED)]
-        z_bf = [keep.tile([P, WIDE, PACK], BF16, name=f"z_bf{pair}", align_bytes=64) for pair in range(PAIRS)]
+        z_bf = [keep.tile([P, WIDE, PACK], BF16, name=f"z_bf{pair}", align_bytes=64) for pair in range(TURNED_PAIRS)]
         fetched = keep.tile([P, TILES, WIDE], F32, name="fetched", align_bytes=64)
         for t in range(TILES):
             nc.scalar.activation(fetched[:, t, :], h[t][:].indirect(pos_sb[:, TAIL // LIST : S // LIST]), ACT.Copy)
@@ -237,13 +230,6 @@ def tile_picked_mixup_gelu_p_kernel(
                 mu_tail[:, c0 : c0 + P].unsqueeze(1).to_broadcast([P, TILES, P]),
                 ALU.mult,
             )
-        for c0 in range(0, WIDE, P):
-            nc.vector.tensor_tensor(
-                z_bf[LAST_PAIR][:, c0 : c0 + P, :].rearrange("p (c i) t -> p c t i", i=4),
-                terms[:, 0, :, c0 : c0 + P].rearrange("p t (c i) -> p c t i", i=4),
-                terms[:, 1, :, c0 : c0 + P].rearrange("p t (c i) -> p c t i", i=4),
-                ALU.add,
-            )
 
         for pair in range(TURNED_PAIRS):
             back = psum.tile([P, 2, 2, P], F32, name="back", tag=f"bank{pair}")
@@ -254,27 +240,38 @@ def tile_picked_mixup_gelu_p_kernel(
             z_words = z_bf[pair][:].rearrange("p s t -> p (s t)").bitcast(F32).rearrange("p (b s u) -> p b s u", b=2, u=2)
             nc.scalar.copy(z_words, back[:].rearrange("p b u s -> p b s u"))
 
-        def second_layer(pair, codes_tag, copy, queue):
-            z_codes = keep.tile([P, WIDE], U32, name=f"z_codes{pair}", tag=codes_tag, align_bytes=64)
+        def second_layer(pair, parts, copy):
+            z_codes = keep.tile([P, WIDE], U32, name=f"z_codes{pair}", align_bytes=64)
             z_scale = keep.tile([P, WIDE], U8, name=f"z_scale{pair}", align_bytes=64)
-            nc.vector.quantize_mx(
-                out=z_codes[:].bitcast(FP8X4), scales=z_scale[:], in_=z_bf[pair][:].rearrange("p c t -> p (c t)")
-            )
-            acc = psum.tile([P, BANK], F32, name="acc", tag=f"bank{4 + pair}")
-            nc.tensor.matmul_mx(
-                out=acc[:, 0:WIDE],
-                lhsT=w2_codes[:].bitcast(FP8X4),
-                lhsT_scale=w2_scale[:],
-                rhs=z_codes[:].bitcast(FP8X4),
-                rhs_scale=z_scale[:],
-                start=True,
-                stop=True,
-            )
             result = keep.tile([P, WIDE], F32, name=f"result{pair}")
-            copy(result[:], acc[:, 0:WIDE])
-            queue.dma_start(out[:, pair * WIDE : (pair + 1) * WIDE], result[:])
+            for (c0, c1), bank in parts:
+                nc.vector.quantize_mx(
+                    out=z_codes[:, c0:c1].bitcast(FP8X4),
+                    scales=z_scale[:, c0:c1],
+                    in_=z_bf[pair][:, c0:c1, :].rearrange("p c t -> p (c t)"),
+                )
+                acc = psum.tile([P, BANK], F32, name="acc", tag=f"bank{bank}")
+                nc.tensor.matmul_mx(
+                    out=acc[:, c0:c1],
+                    lhsT=w1_codes[:, H : H + N].bitcast(FP8X4),
+                    lhsT_scale=w1_scale[:, H : H + N],
+                    rhs=z_codes[:, c0:c1].bitcast(FP8X4),
+                    rhs_scale=z_scale[:, c0:c1],
+                    start=True,
+                    stop=True,
+                )
+                copy(result[:, c0:c1], acc[:, c0:c1])
+            nc.sync.dma_start(out[:, pair * WIDE : (pair + 1) * WIDE], result[:])
 
-        second_layer(0, "z_codes0", nc.scalar.copy, nc.sync)
-        second_layer(LAST_PAIR, f"z_rows{TURNED - 1}", nc.scalar.copy, nc.sync)
-        second_layer(1, "z_codes1", nc.vector.tensor_copy, nc.sync)
-        second_layer(2, "z_codes2", nc.scalar.copy, nc.sync)
+        second_layer(0, (((0, WIDE), 4),), nc.scalar.copy)
+        z_bf.append(keep.tile([P, WIDE, PACK], BF16, name="z_last", tag="z_rows3", align_bytes=64))
+        for c0 in range(0, WIDE, P):
+            nc.vector.tensor_tensor(
+                z_bf[LAST_PAIR][:, c0 : c0 + P, :].rearrange("p (c i) t -> p c t i", i=4),
+                terms[:, 0, :, c0 : c0 + P].rearrange("p t (c i) -> p c t i", i=4),
+                terms[:, 1, :, c0 : c0 + P].rearrange("p t (c i) -> p c t i", i=4),
+                ALU.add,
+            )
+        second_layer(1, (((0, WIDE), 5),), nc.scalar.copy)
+        second_layer(LAST_PAIR, (((0, WIDE), 7),), nc.vector.tensor_copy)
+        second_layer(2, (((0, P), 6), ((P, WIDE), 3)), nc.scalar.copy)

@@ -76,10 +76,8 @@ def tile_picked_mixup_gelu_p_kernel(
         load_w1(0)
         nc.sync.dma_start(lam_runs[:], lam[0].rearrange("(p c) -> p c", c=RUN))
         nc.sync.dma_start(offs_sb[:], offs)
-        for q in range(4):
-            nc.sync.dma_start(
-                scales_all[32 * q : 32 * q + 4, :].bitcast(I32), x_scales[0, 4 * q : 4 * q + 4, :].bitcast(I32)
-            )
+        for r in range(4):
+            nc.sync.dma_start(scales_all[r:P:32, :].bitcast(I32), x_scales[0, r:16:4, :].bitcast(I32))
         nc.sync.dma_start(words_all[:].bitcast(I32), x_words[0].rearrange("p n t -> p (n t)").bitcast(I32))
         nc.sync.dma_start(mu_runs[:], mu[0].rearrange("(p c) -> p c", c=RUN))
         load_w1(1)

@@ -114,7 +114,8 @@ def tile_picked_mixup_gelu_p_kernel(
         for c in range(RUN):
             nc.scalar.activation(ratio_runs[:, c : c + 1], mu_runs[:, c : c + 1], ACT.Copy, scale=inv_runs[:, c : c + 1])
         round_w1(1, 0, 2, nc.scalar.copy)
-        round_w1(2, 0, TILES, nc.scalar.copy)
+        round_w1(2, 0, 2, nc.scalar.copy)
+        round_w1(2, 2, TILES, nc.scalar.copy)
 
         x_scale = keep.tile([P, S], U8, name="x_scale", align_bytes=64)
         x_head = keep.tile([P, WORD_CUT], U32, name="x_head", align_bytes=64)

@@ -192,34 +192,48 @@ def tile_picked_mixup_gelu_p_kernel(
                     partner[t][:, c0:c1], h[t][:].indirect(pos_sb[:, c0 // LIST : c1 // LIST]), ratio[:, c0:c1], ALU.mult
                 )
 
-        def mix_turned(pair, u, terms):
-            sums = psum.tile([P, 2, 2, P], F32, name="sums", tag=f"bank{4 * u + pair}")
-            for i, (source, t) in enumerate(terms):
-                for half in range(2):
-                    b = 2 * pair + half
-                    nc.tensor.matmul(
-                        sums[:, half, t % 2, :],
-                        source[t][:, b * P : (b + 1) * P],
-                        ident[:],
-                        start=(i == 0 and half == 0),
-                        stop=(i == len(terms) - 1 and half == 1),
-                        is_transpose=True,
-                    )
+        sums = [
+            [psum.tile([P, 2, 2, P], F32, name=f"sums{u}{pair}", tag=f"bank{4 * u + pair}") for pair in range(TURNED_PAIRS)]
+            for u in range(2)
+        ]
+
+        def turn(source, t, pair, opens=False, closes=False):
+            for half in range(2):
+                b = 2 * pair + half
+                nc.tensor.matmul(
+                    sums[t // 2][pair][:, half, t % 2, :],
+                    source[t][:, b * P : (b + 1) * P],
+                    ident[:],
+                    start=(opens and half == 0),
+                    stop=(closes and half == 1),
+                    is_transpose=True,
+                )
+
+        def scale(pair, u):
             for half in range(2):
                 b = 2 * pair + half
                 nc.scalar.activation(
                     z_rows[b][:, u, :, :],
-                    sums[:, half, :, :].rearrange("s e p -> s p e"),
+                    sums[u][pair][:, half, :, :].rearrange("s e p -> s p e"),
                     ACT.Copy,
                     scale=own_cols[:, b : b + 1],
                 )
 
         for pair in range(TURNED_PAIRS):
-            mix_turned(pair, 0, ((partner, 1), (h, 0), (h, 1), (partner, 0)))
+            turn(h, 1, pair, opens=True)
+            turn(h, 0, pair)
+        for source, t in ((partner, 0), (h, 2), (h, 3)):
+            for pair in range(TURNED_PAIRS):
+                turn(source, t, pair, opens=(t == 2))
         for pair in range(TURNED_PAIRS):
-            mix_turned(pair, 1, ((partner, 2), (h, 2), (h, 3), (partner, 3)))
+            turn(partner, 1, pair, closes=True)
+            scale(pair, 0)
+        for pair in range(TURNED_PAIRS):
+            turn(partner, 2, pair)
+            turn(partner, 3, pair, closes=True)
+            scale(pair, 1)
 
-        terms = keep.tile([P, 2, TILES, WIDE], F32, name="terms", tag="partner0", align_bytes=64)
+        terms = keep.tile([P, 2, TILES, WIDE], F32, name="terms", tag="partner1", align_bytes=64)
         for t in range(TILES):
             nc.vector.tensor_tensor(terms[:, 0, t, :], h[t][:, TAIL:S], lam_tail[:], ALU.mult)
         for c0 in range(0, WIDE, P):

@@ -28,7 +28,7 @@ TURNED = 6
 TURNED_PAIRS = TURNED // 2
 LAST_PAIR = PAIRS - 1
 TAIL = TURNED * P
-W1_PIECES = ((0, 48), (48, 96), (96, 128))
+W1_PIECES = ((0, 32), (32, 96), (96, 128))
 WORD_CUT = 768
 FIRST_WIDTH = 256
 GATHERS = (((0, TAIL),), ((0, 2 * WIDE), (2 * WIDE, TAIL)), ((0, TAIL),), ((0, WIDE), (WIDE, 2 * WIDE), (2 * WIDE, TAIL)))

from contextlib import ExitStack

import concourse.mybir as mybir

K, T, S, H, N = 512, 2048, 1024, 512, 128
FLOPS = 2 * K * H * S + 2 * H * N * S
BYTES = K * T + 16 * T + 4 * K * H + 4 * H * N + 2 * 4 * S + 2 * 2 * 128 * (S // 16) + 4 * N * S

F32 = mybir.dt.float32
BF16 = mybir.dt.bfloat16
I32 = mybir.dt.int32
U32 = mybir.dt.uint32
U16 = mybir.dt.uint16
U8 = mybir.dt.uint8
FP8X4 = mybir.dt.float8_e4m3fn_x4
ACT = mybir.ActivationFunctionType
ALU = mybir.AluOpType

P = 128
PACK = 4
BANK = 512
LIST = 16
TILES = H // P
RUN = S // P
WIDE = 2 * P
PAIRS = S // WIDE
TURNED = 6
TURNED_PAIRS = TURNED // 2
LAST_PAIR = PAIRS - 1
TAIL = TURNED * P
W1_PIECES = ((0, 32), (32, 96), (96, 128))
WORD_CUT = 768
FIRST_WIDTH = 256
GATHERS = (((0, TAIL),), ((0, 2 * WIDE), (2 * WIDE, TAIL)), ((0, TAIL),), ((0, WIDE), (WIDE, 2 * WIDE), (2 * WIDE, TAIL)))
NUDGES = (2.0**-60, 2.0**-100)


def tile_picked_mixup_gelu_p_kernel(
    tc, x_words, x_scales, w1, w2, lam, mu, offs, pos1, out
):
    nc = tc.nc
    with ExitStack() as ctx:
        keep = ctx.enter_context(tc.tile_pool(name="keep", bufs=1))
        late = ctx.enter_context(tc.tile_pool(name="late", bufs=1))
        psum = ctx.enter_context(tc.psum_pool(name="psum", bufs=1))

        offs_sb = keep.tile([P, S // LIST], U16, name="offs_sb")
        pos_sb = keep.tile([P, S // LIST], U16, name="pos_sb")
        words_all = keep.tile([P, T], U32, name="words_all", align_bytes=64)
        scales_all = keep.tile([P, T], U8, name="scales_all", align_bytes=64)
        w1_raw = [keep.tile([P, PACK, PACK * (m1 - m0)], F32, name=f"w1_raw{m0}", align_bytes=64) for m0, m1 in W1_PIECES[:2]]
        w1_raw.append(late.tile([P, PACK, PACK * (W1_PIECES[2][1] - W1_PIECES[2][0])], F32, name="w1_last", offset=0, align_bytes=64))
        w2_raw = keep.tile([P, PACK, N], F32, name="w2_raw")
        lam_cols = keep.tile([P, TURNED], F32, name="lam_cols")
        lam_runs = keep.tile([P, RUN], F32, name="lam_runs")
        mu_runs = keep.tile([P, RUN], F32, name="mu_runs")
        lam_tail = keep.tile([P, WIDE], F32, name="lam_tail")
        mu_tail = keep.tile([P, WIDE], F32, name="mu_tail")
        ident = keep.tile([P, P], F32, name="ident")
        ones = keep.tile([P, P], F32, name="ones")
        base = keep.tile([P, 1], F32, name="base")
        counts = keep.tile([P, P], F32, name="counts", align_bytes=64)
        row_number = keep.tile([P, 32], F32, name="row_number", align_bytes=64)
        warm = keep.tile([P, 1], F32, name="warm")

        nc.vector.memset(scales_all[:].bitcast(I32), 0)
        nc.vector.memset(ones[:], 1.0)
        nc.scalar.activation(warm[:], ones[:, 0:1], ACT.Gelu_apprx_tanh)

        w1_view = w1.rearrange("(p j) c -> p j c", j=PACK)

        def load_w1(i):
            m0, m1 = W1_PIECES[i]
            nc.sync.dma_start(w1_raw[i][:], w1_view[:, :, PACK * m0 : PACK * m1])

        load_w1(0)
        nc.sync.dma_start(lam_runs[:], lam[0].rearrange("(p c) -> p c", c=RUN))
        nc.sync.dma_start(offs_sb[:], offs)
        for r in range(4):
            nc.sync.dma_start(scales_all[r:P:32, :].bitcast(I32), x_scales[0, r:16:4, :].bitcast(I32))
        nc.sync.dma_start(words_all[:].bitcast(I32), x_words[0].rearrange("p n t -> p (n t)").bitcast(I32))
        nc.sync.dma_start(mu_runs[:], mu[0].rearrange("(p c) -> p c", c=RUN))
        load_w1(1)
        load_w1(2)
        nc.sync.dma_start(pos_sb[:], pos1)
        nc.sync.dma_start(w2_raw[:], w2.rearrange("(p j) c -> p j c", j=PACK))
        with nc.allow_non_contiguous_dma(reason="one value a partition and block"):
            nc.sync.dma_start(lam_cols[:], lam[0, 0:TAIL].rearrange("(b s) -> s b", s=P))
        nc.sync.dma_start(lam_tail[:], lam[:, TAIL:S])
        nc.sync.dma_start(mu_tail[:], mu[:, TAIL:S])

        for q in range(4):
            nc.vector.memset(base[32 * q : 32 * q + 32, :], 32.0 * q)
        nc.vector.tensor_tensor_scan(counts[:], ones[:], ones[:], base[:], ALU.mult, ALU.add)
        nc.vector.transpose(row_number[:], counts[:, 0:32])
        nc.vector.tensor_scalar(ident[:], counts[:], base[:], row_number[:, 0:1], ALU.subtract, ALU.is_equal)

        own_runs = keep.tile([P, RUN], F32, name="own_runs")
        inv_runs = keep.tile([P, RUN], F32, name="inv_runs")
        ratio_runs = keep.tile([P, RUN], F32, name="ratio_runs")
        nc.vector.tensor_scalar(own_runs[:], lam_runs[:], NUDGES[0], NUDGES[1], ALU.add, ALU.add)
        nc.vector.reciprocal(inv_runs[:], own_runs[:])

        w1_bf = keep.tile([P, TILES + 1, P, PACK], BF16, name="w1_bf", align_bytes=64)

        def round_w1(i, t0, t1, copy):
            m0, m1 = W1_PIECES[i]
            copy(
                w1_bf[:, t0:t1, m0:m1, :].rearrange("p t m j -> p m j t"),
                w1_raw[i][:].rearrange("p j (m t) -> p m j t", t=PACK)[:, :, :, t0:t1],
            )

        round_w1(0, 0, TILES, nc.scalar.copy)
        for c in range(RUN):
            nc.scalar.activation(ratio_runs[:, c : c + 1], mu_runs[:, c : c + 1], ACT.Copy, scale=inv_runs[:, c : c + 1])
        round_w1(1, 0, 2, nc.scalar.copy)
        round_w1(2, 0, 2, nc.scalar.copy)
        round_w1(2, 2, TILES, nc.scalar.copy)

        x_scale = keep.tile([P, S], U8, name="x_scale", align_bytes=64)
        x_head = keep.tile([P, WORD_CUT], U32, name="x_head", align_bytes=64)
        nc.vector.tensor_copy(x_scale[:], scales_all[:].indirect(offs_sb[:]))
        nc.vector.tensor_copy(x_head[:], words_all[:].indirect(offs_sb[:, 0 : WORD_CUT // LIST]))

        ratio = late.tile([P, TAIL], F32, name="ratio", offset=4 * (S - WORD_CUT), align_bytes=64)
        per_bank = BANK // P
        for bank in range(RUN // per_bank):
            spread = psum.tile([P, per_bank, P], F32, name="spread", tag=f"bank{bank}")
            for i in range(per_bank):
                c = bank * per_bank + i
                nc.tensor.transpose(spread[:, i, :], ratio_runs[:, c : c + 1].to_broadcast([P, P]), ident[:])
            nc.scalar.copy(
                ratio[:].rearrange("q (n c) -> q n c", c=RUN)[:, :, bank * per_bank : (bank + 1) * per_bank],
                spread[:, :, 0 : TAIL // RUN].rearrange("q i n -> q n i"),
            )

        w1_codes = keep.tile([P, H + N], U32, name="w1_codes", align_bytes=64)
        w1_scale = keep.tile([P, H + N], U8, name="w1_scale", align_bytes=64)

        def quantise_w1(t0, t1):
            nc.vector.quantize_mx(
                out=w1_codes[:, t0 * P : t1 * P].bitcast(FP8X4),
                scales=w1_scale[:, t0 * P : t1 * P],
                in_=w1_bf[:, t0:t1, :, :].rearrange("p t m j -> p (t m j)"),
            )

        quantise_w1(0, 1)
        x_rest = late.tile([P, S - WORD_CUT], U32, name="x_rest", offset=0, align_bytes=64)
        nc.vector.tensor_copy(x_rest[:], words_all[:].indirect(offs_sb[:, WORD_CUT // LIST : S // LIST]))
        quantise_w1(1, 2)
        round_w1(1, 2, TILES, nc.vector.tensor_copy)
        nc.vector.tensor_copy(
            w1_bf[:, TILES, :, :].rearrange("p (c i) j -> p c j i", i=4), w2_raw[:].rearrange("p j (c i) -> p c j i", i=4)
        )
        own_cols = keep.tile([P, TURNED], F32, name="own_cols")
        nc.vector.tensor_scalar(own_cols[:], lam_cols[:], NUDGES[0], NUDGES[1], ALU.add, ALU.add)
        quantise_w1(2, TILES + 1)

        h = [keep.tile([P, S], F32, name=f"h{t}", align_bytes=64) for t in range(TILES)]

        def first_layer(t, c0, c1, bank):
            acc = psum.tile([P, BANK], F32, name="acc", tag=f"bank{bank}")
            cuts = (c0, WORD_CUT, c1) if c0 < WORD_CUT < c1 else (c0, c1)
            for a, b in zip(cuts, cuts[1:]):
                codes = x_head[:, a:b] if b <= WORD_CUT else x_rest[:, a - WORD_CUT : b - WORD_CUT]
                nc.tensor.matmul_mx(
                    out=acc[:, a - c0 : b - c0],
                    lhsT=w1_codes[:, t * P : (t + 1) * P].bitcast(FP8X4),
                    lhsT_scale=w1_scale[:, t * P : (t + 1) * P],
                    rhs=codes.bitcast(FP8X4),
                    rhs_scale=x_scale[:, a:b],
                    start=True,
                    stop=True,
                )
            nc.scalar.activation(h[t][:, c0:c1], acc[:, 0 : c1 - c0], ACT.Gelu_apprx_tanh)

        for i, bank in enumerate((5, 6, 7, 4)):
            first_layer(0, i * FIRST_WIDTH, (i + 1) * FIRST_WIDTH, bank)
        for i in range(2 * (TILES - 1)):
            first_layer(1 + i // 2, i % 2 * BANK, (i % 2 + 1) * BANK, 5 + i % 3)

        partner = [keep.tile([P, TAIL], F32, name=f"partner{t}", tag=f"partner{t}", align_bytes=64) for t in range(TILES)]
        z_rows = [keep.tile([P, 2, P, 2], BF16, name=f"z_rows{b}", tag=f"z_rows{b}", align_bytes=64) for b in range(TURNED)]
        z_bf = [keep.tile([P, WIDE, PACK], BF16, name=f"z_bf{pair}", align_bytes=64) for pair in range(TURNED_PAIRS)]
        fetched = keep.tile([P, TILES, WIDE], F32, name="fetched", align_bytes=64)
        for t in range(TILES):
            nc.scalar.activation(fetched[:, t, :], h[t][:].indirect(pos_sb[:, TAIL // LIST : S // LIST]), ACT.Copy)

        for t in range(TILES):
            for c0, c1 in GATHERS[t]:
                nc.vector.tensor_tensor(
                    partner[t][:, c0:c1], h[t][:].indirect(pos_sb[:, c0 // LIST : c1 // LIST]), ratio[:, c0:c1], ALU.mult
                )

        sums = [
            [psum.tile([P, 2, 2, P], F32, name=f"sums{u}{pair}", tag=f"bank{4 * u + pair}") for pair in range(TURNED_PAIRS)]
            for u in range(2)
        ]

        def turn(source, t, pair, opens=False, closes=False):
            for half in range(2):
                b = 2 * pair + half
                nc.tensor.matmul(
                    sums[t // 2][pair][:, half, t % 2, :],
                    source[t][:, b * P : (b + 1) * P],
                    ident[:],
                    start=(opens and half == 0),
                    stop=(closes and half == 1),
                    is_transpose=True,
                )

        def scale(pair, u):
            for half in range(2):
                b = 2 * pair + half
                nc.scalar.activation(
                    z_rows[b][:, u, :, :],
                    sums[u][pair][:, half, :, :].rearrange("s e p -> s p e"),
                    ACT.Copy,
                    scale=own_cols[:, b : b + 1],
                )

        for pair in range(TURNED_PAIRS):
            turn(h, 1, pair, opens=True)
            turn(h, 0, pair)
        for source, t in ((partner, 0), (h, 2), (h, 3)):
            for pair in range(TURNED_PAIRS):
                turn(source, t, pair, opens=(t == 2))
        for pair in range(TURNED_PAIRS):
            turn(partner, 1, pair, closes=True)
            scale(pair, 0)
        for pair in range(TURNED_PAIRS):
            turn(partner, 2, pair)
            turn(partner, 3, pair, closes=True)
            scale(pair, 1)

        terms = keep.tile([P, 2, TILES, WIDE], F32, name="terms", tag="partner1", align_bytes=64)
        for t in range(TILES):
            nc.vector.tensor_tensor(terms[:, 0, t, :], h[t][:, TAIL:S], lam_tail[:], ALU.mult)
        for c0 in range(0, WIDE, P):
            nc.vector.tensor_tensor(
                terms[:, 1, :, c0 : c0 + P],
                fetched[:, :, c0 : c0 + P],
                mu_tail[:, c0 : c0 + P].unsqueeze(1).to_broadcast([P, TILES, P]),
                ALU.mult,
            )

        for pair in range(TURNED_PAIRS):
            back = psum.tile([P, 2, 2, P], F32, name="back", tag=f"bank{pair}")
            for half in range(2):
                words = z_rows[2 * pair + half][:].rearrange("s u p e -> s (u p e)").bitcast(F32)
                for u in range(2):
                    nc.tensor.transpose(back[:, half, u, :], words[:, u * P : (u + 1) * P], ident[:])
            z_words = z_bf[pair][:].rearrange("p s t -> p (s t)").bitcast(F32).rearrange("p (b s u) -> p b s u", b=2, u=2)
            nc.scalar.copy(z_words, back[:].rearrange("p b u s -> p b s u"))

        def second_layer(pair, parts, copy):
            z_codes = keep.tile([P, WIDE], U32, name=f"z_codes{pair}", align_bytes=64)
            z_scale = keep.tile([P, WIDE], U8, name=f"z_scale{pair}", align_bytes=64)
            result = keep.tile([P, WIDE], F32, name=f"result{pair}")
            for (c0, c1), bank in parts:
                nc.vector.quantize_mx(
                    out=z_codes[:, c0:c1].bitcast(FP8X4),
                    scales=z_scale[:, c0:c1],
                    in_=z_bf[pair][:, c0:c1, :].rearrange("p c t -> p (c t)"),
                )
                acc = psum.tile([P, BANK], F32, name="acc", tag=f"bank{bank}")
                nc.tensor.matmul_mx(
                    out=acc[:, c0:c1],
                    lhsT=w1_codes[:, H : H + N].bitcast(FP8X4),
                    lhsT_scale=w1_scale[:, H : H + N],
                    rhs=z_codes[:, c0:c1].bitcast(FP8X4),
                    rhs_scale=z_scale[:, c0:c1],
                    start=True,
                    stop=True,
                )
                copy(result[:, c0:c1], acc[:, c0:c1])
            nc.sync.dma_start(out[:, pair * WIDE : (pair + 1) * WIDE], result[:])

        second_layer(0, (((0, WIDE), 4),), nc.scalar.copy)
        z_bf.append(keep.tile([P, WIDE, PACK], BF16, name="z_last", tag="z_rows3", align_bytes=64))
        for c0 in range(0, WIDE, P):
            nc.vector.tensor_tensor(
                z_bf[LAST_PAIR][:, c0 : c0 + P, :].rearrange("p (c i) t -> p c t i", i=4),
                terms[:, 0, :, c0 : c0 + P].rearrange("p t (c i) -> p c t i", i=4),
                terms[:, 1, :, c0 : c0 + P].rearrange("p t (c i) -> p c t i", i=4),
                ALU.add,
            )
        second_layer(1, (((0, WIDE), 5),), nc.scalar.copy)
        second_layer(LAST_PAIR, (((0, WIDE), 7),), nc.vector.tensor_copy)
        second_layer(2, (((0, P), 6), ((P, WIDE), 3)), nc.scalar.copy)
